import numpy as np
import ml_dtypes


def mxq(x, axis, fmt="e4m3"):
    dtype, down = {"e4m3": (ml_dtypes.float8_e4m3fn, 7), "e5m2": (ml_dtypes.float8_e5m2, 14)}[fmt]
    v = np.moveaxis(np.asarray(x, np.float32).astype(ml_dtypes.bfloat16).astype(np.float64), axis, -1)
    blocks = v.reshape(v.shape[:-1] + (-1, 32))
    amax = np.abs(blocks).max(-1, keepdims=True)
    byte = np.maximum(np.where(amax > 0, np.frexp(amax)[1] - 1 + 127, 0) - down, 1)
    scale = np.exp2(byte - 127.0)
    codes = (blocks / scale).astype(np.float32).astype(dtype).astype(np.float64)
    return np.moveaxis((codes * scale).reshape(v.shape), -1, axis)


WIDE = False


def mx_kscale(k):
    if not WIDE:
        return np.ones(k)
    levels = np.array([24, -24, 12, -12, 0])
    if k % 512:
        return np.exp2(np.random.permutation(np.resize(levels, k // 32))).repeat(32)
    a = np.empty((k // 512, 16))
    for p in range(k // 512):
        a[p, :8] = np.random.permutation(np.resize(levels, 8))
        for g in range(8):
            far = levels[np.abs(levels - a[p, g]) >= 10]
            a[p, g + 8] = far[np.random.randint(len(far))]
    return np.exp2(a.ravel()).repeat(32)


def f64(x):
    return np.asarray(x).astype(np.float64)


def striped8(idx):
    return np.concatenate([v.reshape(-1, 16).T for v in idx]).astype(np.uint16)


def unstriped8(offs):
    return np.stack([offs[16 * g:16 * g + 16].T.reshape(-1) for g in range(8)]).astype(np.int64)


E2M1 = np.array([0.0, 0.5, 1.0, 1.5, 2.0, 3.0, 4.0, 6.0, -0.0, -0.5, -1.0, -1.5, -2.0, -3.0, -4.0, -6.0])


def pack_weight(w, fmt):
    k, n = w.shape
    w = f64(np.asarray(w, np.float32).astype(ml_dtypes.bfloat16)).reshape(k // 32, 32, n)
    amax = np.abs(w).max(1)
    if fmt == "e4m3":
        byte = np.frexp(amax)[1] - 1 + 127 - 7
    else:
        mant, ex = np.frexp(amax / 6.0)
        byte = np.where(mant > 0.5, ex, ex - 1) + 127
    byte = np.clip(np.where(amax > 0, byte, 1), 1, 254)
    scaled = (w * np.exp2(127.0 - byte)[:, None, :]).reshape(k, n).astype(np.float32)
    by_word = np.ascontiguousarray(scaled.reshape(k // 512, 128, 4, n).transpose(0, 1, 3, 2))
    if fmt == "e4m3":
        words = by_word.astype(ml_dtypes.float8_e4m3fn).view(np.uint8)
    else:
        c = by_word.astype(ml_dtypes.float4_e2m1fn).view(np.uint8) & 0xF
        words = (c[..., 0::2] | (c[..., 1::2] << 4)).reshape(k // 512, 128, 2 * n)
    return np.ascontiguousarray(words), np.ascontiguousarray(byte.astype(np.uint8).reshape(k // 512, 16, n))


def unpack_weight(words, scales, fmt):
    g, _, n = scales.shape
    words = np.ascontiguousarray(words).reshape(g, 128, n, -1)
    if fmt == "e4m3":
        vals = words.view(ml_dtypes.float8_e4m3fn).astype(np.float64)
    else:
        nib = np.empty((g, 128, n, 4), np.uint8)
        nib[..., 0::2] = words & 0xF
        nib[..., 1::2] = words >> 4
        vals = E2M1[nib]
    vals = vals * np.repeat(np.exp2(scales.astype(np.float64) - 127.0), 8, axis=1)[..., None]
    return vals.transpose(0, 1, 3, 2).reshape(g * 512, n)


K, N, T, J = 512, 512, 2048, 512


def setup_inputs():
    n = np.random.standard_normal
    s = mx_kscale(K)[:, None]
    p_w = pack_weight(n((K, N)) / np.sqrt(K) / s, "e2m1")
    return {
        "xT": (n((K, T)) * s).astype(np.float32),
        "wgt": np.repeat(np.random.uniform(0.5, 2.0, (8, 3 * J)), 16, axis=0).astype(np.float32),
        "w_words": p_w[0],
        "w_scales": p_w[1],
        "b": (0.3 * n(N)).astype(np.float32),
        "offs": striped8(np.stack([np.concatenate([np.random.permutation(T)[:J] for _ in range(3)]) for _ in range(8)])),
    }


def reference(xT, wgt, w_words, w_scales, b, offs):
    idx = unstriped8(offs)
    rows = np.arange(K)
    xg = f64(wgt)[rows // 4 % 128] * f64(xT)[rows[:, None], idx[rows % 512 // 64]]
    xT_ = mxq(xg, 0, "e4m3").reshape(K, 3, J)
    w_ = unpack_weight(w_words, w_scales, "e2m1")
    a0 = w_.T @ xT_[:, 0]
    a1 = w_.T @ xT_[:, 1]
    a2 = w_.T @ xT_[:, 2]
    return np.maximum(np.maximum(a0, a1), a2) + f64(b)[:, None]

@@ -1,0 +1,106 @@
+from contextlib import ExitStack
+
+import concourse.mybir as mybir
+
+K, N, T, J, PICKS = 512, 512, 2048, 512, 3
+FLOPS = 2 * K * N * J * PICKS
+
+F32 = mybir.dt.float32
+BF16 = mybir.dt.bfloat16
+I32 = mybir.dt.int32
+U32 = mybir.dt.uint32
+U16 = mybir.dt.uint16
+U8 = mybir.dt.uint8
+FP8X4 = mybir.dt.float8_e4m3fn_x4
+FP4X4 = mybir.dt.float4_e2m1fn_x4
+ALU = mybir.AluOpType
+ACT = mybir.ActivationFunctionType
+P = 128
+PACK = 4
+
+
+def tile_list_max_bias_kernel(tc, xT, wgt, w_words, w_scales, b, offs, out):
+    nc = tc.nc
+    with ExitStack() as ctx:
+        keep = ctx.enter_context(tc.tile_pool(name="keep", bufs=1))
+        psum = ctx.enter_context(tc.psum_pool(name="psum", bufs=2))
+
+        offsets = keep.tile([P, PICKS * J // 16], U16, name="offsets")
+        nc.sync.dma_start(offsets[:], offs)
+        w_scale = keep.tile([P, N], U8, name="w_scale", align_bytes=64)
+        nc.gpsimd.memset(w_scale[:].bitcast(I32), 0)
+
+        x_planes = xT.rearrange("(p i) t -> p i t", i=PACK)
+        plane = [keep.tile([P, T], F32, name=f"plane{i}") for i in range(PACK)]
+        weight = [keep.tile([P, J], F32, name=f"weight{c}") for c in range(PICKS)]
+        nc.sync.dma_start(plane[0][:], x_planes[:, 0, :])
+        nc.sync.dma_start(weight[0][:], wgt[:, 0:J])
+        nc.sync.dma_start(weight[1][:], wgt[:, J:2 * J])
+        nc.sync.dma_start(plane[1][:], x_planes[:, 1, :])
+        nc.sync.dma_start(plane[2][:], x_planes[:, 2, :])
+        nc.sync.dma_start(plane[3][:], x_planes[:, 3, :])
+        nc.sync.dma_start(weight[2][:], wgt[:, 2 * J:3 * J])
+        w_codes = keep.tile([P, 2 * N], U8, name="w_codes", align_bytes=64)
+        nc.sync.dma_start(w_codes[:].bitcast(I32), w_words[0].bitcast(I32))
+        for q in range(4):
+            nc.sync.dma_start(w_scale[32 * q:32 * q + 4, :].bitcast(I32), w_scales[0, 4 * q:4 * q + 4, :].bitcast(I32))
+        bias = keep.tile([P, N // P], F32, name="bias")
+        with nc.allow_non_contiguous_dma(reason="one bias value a partition"):
+            nc.sync.dma_start(bias[:], b.rearrange("(m p) -> p m", p=P))
+
+        picked = [keep.tile([P, PACK, J], F32, name=f"picked{c}") for c in range(PICKS)]
+        grouped = [keep.tile([P, J, PACK], BF16, name=f"grouped{c}", align_bytes=64) for c in range(PICKS)]
+        codes = [keep.tile([P, J], U32, name=f"codes{c}", align_bytes=64) for c in range(PICKS)]
+        scales = [keep.tile([P, J], U8, name=f"scales{c}", align_bytes=64) for c in range(PICKS)]
+        pooled = [[keep.tile([P, J], F32, name=f"pooled{c}_{m}") for m in range(N // P)] for c in range(PICKS)]
+        acc = {}
+
+        def gather(c, i):
+            nc.vector.tensor_tensor(picked[c][:, i, :], plane[i][:].indirect(offsets[:, c * J // 16:(c + 1) * J // 16]), weight[c][:], ALU.mult)
+
+        def interleave(c):
+            for h in range(2):
+                js = slice(h * J // 2, (h + 1) * J // 2)
+                nc.scalar.copy(grouped[c][:, js, :], picked[c][:, :, js].rearrange("p i j -> p j i"))
+
+        def quantize(c):
+            nc.vector.quantize_mx(out=codes[c][:].bitcast(FP8X4), scales=scales[c][:], in_=grouped[c][:].rearrange("p j i -> p (j i)"))
+
+        def project(c):
+            for m in range(N // P):
+                acc[c, m] = psum.tile([P, J], F32, name=f"acc{m}")
+                nc.tensor.matmul_mx(out=acc[c, m][:], lhsT=w_codes[:, 2 * P * m:2 * P * (m + 1)].bitcast(FP4X4),
+                                    lhsT_scale=w_scale[:, P * m:P * (m + 1)], rhs=codes[c][:].bitcast(FP8X4),
+                                    rhs_scale=scales[c][:], start=True, stop=True)
+
+        def pool(c, m):
+            if c == 0:
+                nc.scalar.activation(pooled[c][m][:], acc[c, m][:], ACT.Identity, bias=bias[:, m:m + 1])
+            else:
+                nc.vector.scalar_tensor_tensor(pooled[c][m][:], acc[c, m][:], bias[:, m:m + 1], pooled[c - 1][m][:], ALU.add, ALU.max)
+
+        for i in range(PACK):
+            gather(0, i)
+            gather(1, i)
+        interleave(0)
+        interleave(1)
+        gather(2, 0)
+        quantize(0)
+        project(0)
+        for m in range(4):
+            pool(0, m)
+        gather(2, 1)
+        gather(2, 2)
+        quantize(1)
+        project(1)
+        gather(2, 3)
+        interleave(2)
+        pool(1, 0)
+        pool(1, 1)
+        pool(1, 2)
+        quantize(2)
+        project(2)
+        pool(1, 3)
+        for m in range(4):
+            pool(2, m)
+            nc.sync.dma_start(out[P * m:P * (m + 1), :], pooled[2][m][:])

@@ -17,6 +17,8 @@ ALU = mybir.AluOpType
 ACT = mybir.ActivationFunctionType
 P = 128
 PACK = 4
+H = J // 2
+FIRST = 384
 
 
 def tile_list_max_bias_kernel(tc, xT, wgt, w_words, w_scales, b, offs, out):
@@ -26,20 +28,25 @@ def tile_list_max_bias_kernel(tc, xT, wgt, w_words, w_scales, b, offs, out):
         psum = ctx.enter_context(tc.psum_pool(name="psum", bufs=2))
 
         offsets = keep.tile([P, PICKS * J // 16], U16, name="offsets")
-        nc.sync.dma_start(offsets[:], offs)
         w_scale = keep.tile([P, N], U8, name="w_scale", align_bytes=64)
         nc.gpsimd.memset(w_scale[:].bitcast(I32), 0)
 
+        early = keep.tile([P, PACK * 2 * J], F32, name="early")
+        late = keep.tile([P, PACK * 2 * J], F32, name="late", align_bytes=64)
+        weight_late = keep.tile([P, J], F32, name="weight_late")
+        last = keep.tile([P, 2 * J], F32, name="last", align_bytes=64)
+        weight_early = late[:, 2 * J:4 * J]
+        grouped = [late[:, 4 * J:6 * J].bitcast(BF16), late[:, 6 * J:8 * J].bitcast(BF16), last[:].bitcast(BF16)]
+
         x_planes = xT.rearrange("(p i) t -> p i t", i=PACK)
         plane = [keep.tile([P, T], F32, name=f"plane{i}") for i in range(PACK)]
-        weight = [keep.tile([P, J], F32, name=f"weight{c}") for c in range(PICKS)]
         nc.sync.dma_start(plane[0][:], x_planes[:, 0, :])
-        nc.sync.dma_start(weight[0][:], wgt[:, 0:J])
-        nc.sync.dma_start(weight[1][:], wgt[:, J:2 * J])
-        nc.sync.dma_start(plane[1][:], x_planes[:, 1, :])
-        nc.sync.dma_start(plane[2][:], x_planes[:, 2, :])
-        nc.sync.dma_start(plane[3][:], x_planes[:, 3, :])
-        nc.sync.dma_start(weight[2][:], wgt[:, 2 * J:3 * J])
+        nc.sync.dma_start(offsets[:], offs)
+        nc.sync.dma_start(weight_early[:, 0:FIRST], wgt[:, 0:FIRST])
+        nc.sync.dma_start(weight_early[:, FIRST:2 * J], wgt[:, FIRST:2 * J])
+        nc.sync.dma_start(weight_late[:], wgt[:, 2 * J:3 * J])
+        for i in range(1, PACK):
+            nc.sync.dma_start(plane[i][:], x_planes[:, i, :])
         w_codes = keep.tile([P, 2 * N], U8, name="w_codes", align_bytes=64)
         nc.sync.dma_start(w_codes[:].bitcast(I32), w_words[0].bitcast(I32))
         for q in range(4):
@@ -48,59 +55,66 @@ def tile_list_max_bias_kernel(tc, xT, wgt, w_words, w_scales, b, offs, out):
         with nc.allow_non_contiguous_dma(reason="one bias value a partition"):
             nc.sync.dma_start(bias[:], b.rearrange("(m p) -> p m", p=P))
 
-        picked = [keep.tile([P, PACK, J], F32, name=f"picked{c}") for c in range(PICKS)]
-        grouped = [keep.tile([P, J, PACK], BF16, name=f"grouped{c}", align_bytes=64) for c in range(PICKS)]
         codes = [keep.tile([P, J], U32, name=f"codes{c}", align_bytes=64) for c in range(PICKS)]
         scales = [keep.tile([P, J], U8, name=f"scales{c}", align_bytes=64) for c in range(PICKS)]
-        pooled = [[keep.tile([P, J], F32, name=f"pooled{c}_{m}") for m in range(N // P)] for c in range(PICKS)]
+        pooled = {(c, m): keep.tile([P, J], F32, name=f"pooled{c}_{m}")[:] for c in range(PICKS) for m in range(N // P) if (c, m) != (1, 3)}
+        pooled[1, 3] = last[:, 0:J]
         acc = {}
 
-        def gather(c, i):
-            nc.vector.tensor_tensor(picked[c][:, i, :], plane[i][:].indirect(offsets[:, c * J // 16:(c + 1) * J // 16]), weight[c][:], ALU.mult)
+        def gather_early(i, e0, e1):
+            nc.vector.tensor_tensor(early[:, 2 * J * i + e0:2 * J * i + e1], plane[i][:].indirect(offsets[:, e0 // 16:e1 // 16]),
+                                    weight_early[:, e0:e1], ALU.mult)
 
-        def interleave(c):
-            for h in range(2):
-                js = slice(h * J // 2, (h + 1) * J // 2)
-                nc.scalar.copy(grouped[c][:, js, :], picked[c][:, :, js].rearrange("p i j -> p j i"))
+        def gather_late(i, j0, j1):
+            nc.vector.tensor_tensor(late[:, 2 * J * i + j0:2 * J * i + j1], plane[i][:].indirect(offsets[:, (2 * J + j0) // 16:(2 * J + j1) // 16]),
+                                    weight_late[:, j0:j1], ALU.mult)
 
-        def quantize(c):
-            nc.vector.quantize_mx(out=codes[c][:].bitcast(FP8X4), scales=scales[c][:], in_=grouped[c][:].rearrange("p j i -> p (j i)"))
+        def interleave(c, j0, j1):
+            products = early[:] if c < 2 else late[:]
+            e0 = J * (c % 2) + j0
+            src = products.rearrange("p (i q r) -> p q i r", i=PACK, r=4)[:, e0 // 4:(e0 + j1 - j0) // 4]
+            dst = grouped[c][:, PACK * j0:PACK * j1].rearrange("p (q r i) -> p q i r", i=PACK, r=4)
+            nc.scalar.copy(dst, src)
 
-        def project(c):
+        def quantize_and_project(c):
+            nc.vector.quantize_mx(out=codes[c][:].bitcast(FP8X4), scales=scales[c][:], in_=grouped[c])
             for m in range(N // P):
                 acc[c, m] = psum.tile([P, J], F32, name=f"acc{m}")
                 nc.tensor.matmul_mx(out=acc[c, m][:], lhsT=w_codes[:, 2 * P * m:2 * P * (m + 1)].bitcast(FP4X4),
                                     lhsT_scale=w_scale[:, P * m:P * (m + 1)], rhs=codes[c][:].bitcast(FP8X4),
                                     rhs_scale=scales[c][:], start=True, stop=True)
 
-        def pool(c, m):
-            if c == 0:
-                nc.scalar.activation(pooled[c][m][:], acc[c, m][:], ACT.Identity, bias=bias[:, m:m + 1])
-            else:
-                nc.vector.scalar_tensor_tensor(pooled[c][m][:], acc[c, m][:], bias[:, m:m + 1], pooled[c - 1][m][:], ALU.add, ALU.max)
+        def pool(c, m, j0=0, j1=J):
+            nc.vector.scalar_tensor_tensor(pooled[c, m][:, j0:j1], acc[c, m][:, j0:j1], bias[:, m:m + 1], pooled[c - 1, m][:, j0:j1], ALU.add, ALU.max)
 
-        for i in range(PACK):
-            gather(0, i)
-            gather(1, i)
-        interleave(0)
-        interleave(1)
-        gather(2, 0)
-        quantize(0)
-        project(0)
-        for m in range(4):
-            pool(0, m)
-        gather(2, 1)
-        gather(2, 2)
-        quantize(1)
-        project(1)
-        gather(2, 3)
-        interleave(2)
-        pool(1, 0)
-        pool(1, 1)
-        pool(1, 2)
-        quantize(2)
-        project(2)
+        gather_early(0, 0, FIRST)
+        gather_early(0, FIRST, 2 * J)
+        gather_late(0, 0, J)
+        gather_early(1, 0, 2 * J)
+        gather_early(2, 0, 2 * J)
+        gather_early(3, 0, H)
+        interleave(0, 0, H)
+        gather_early(3, H, J)
+        interleave(0, H, J)
+        gather_early(3, J, 2 * J)
+        interleave(1, 0, J)
+        gather_late(1, 0, J)
+        quantize_and_project(0)
+        for m in range(N // P):
+            nc.scalar.activation(pooled[0, m], acc[0, m][:], ACT.Identity, bias=bias[:, m:m + 1])
+        gather_late(2, 0, J)
+        quantize_and_project(1)
+        gather_late(3, 0, H)
+        interleave(2, 0, H)
+        gather_late(3, H, J)
+        interleave(2, H, J)
+        for m in range(3):
+            pool(1, m)
+        quantize_and_project(2)
         pool(1, 3)
-        for m in range(4):
+        for m in range(3):
             pool(2, m)
-            nc.sync.dma_start(out[P * m:P * (m + 1), :], pooled[2][m][:])
+            nc.sync.dma_start(out[P * m:P * (m + 1), :], pooled[2, m])
+        for h, queue in ((0, nc.scalar), (1, nc.sync)):
+            pool(2, 3, h * H, (h + 1) * H)
+            queue.dma_start(out[3 * P:4 * P, h * H:(h + 1) * H], pooled[2, 3][:, h * H:(h + 1) * H])

@@ -19,6 +19,9 @@ P = 128
 PACK = 4
 H = J // 2
 FIRST = 384
+LEAD = 192
+EARLY_PITCH = 15 * J // 4
+LATE_PITCH = 7 * J // 4
 
 
 def tile_list_max_bias_kernel(tc, xT, wgt, w_words, w_scales, b, offs, out):
@@ -31,12 +34,11 @@ def tile_list_max_bias_kernel(tc, xT, wgt, w_words, w_scales, b, offs, out):
         w_scale = keep.tile([P, N], U8, name="w_scale", align_bytes=64)
         nc.gpsimd.memset(w_scale[:].bitcast(I32), 0)
 
-        early = keep.tile([P, PACK * 2 * J], F32, name="early")
-        late = keep.tile([P, PACK * 2 * J], F32, name="late", align_bytes=64)
+        early = keep.tile([P, PACK * EARLY_PITCH], F32, name="early")
+        late = early[:, 2 * EARLY_PITCH - LATE_PITCH:2 * EARLY_PITCH + 3 * LATE_PITCH]
+        weight_early = keep.tile([P, 2 * J], F32, name="weight_early")
         weight_late = keep.tile([P, J], F32, name="weight_late")
-        last = keep.tile([P, 2 * J], F32, name="last", align_bytes=64)
-        weight_early = late[:, 2 * J:4 * J]
-        grouped = [late[:, 4 * J:6 * J].bitcast(BF16), late[:, 6 * J:8 * J].bitcast(BF16), last[:].bitcast(BF16)]
+        grouped = [keep.tile([P, PACK * J], BF16, name=f"grouped{c}", align_bytes=64)[:] for c in range(PICKS)]
 
         x_planes = xT.rearrange("(p i) t -> p i t", i=PACK)
         plane = [keep.tile([P, T], F32, name=f"plane{i}") for i in range(PACK)]
@@ -57,64 +59,101 @@ def tile_list_max_bias_kernel(tc, xT, wgt, w_words, w_scales, b, offs, out):
 
         codes = [keep.tile([P, J], U32, name=f"codes{c}", align_bytes=64) for c in range(PICKS)]
         scales = [keep.tile([P, J], U8, name=f"scales{c}", align_bytes=64) for c in range(PICKS)]
-        pooled = {(c, m): keep.tile([P, J], F32, name=f"pooled{c}_{m}")[:] for c in range(PICKS) for m in range(N // P) if (c, m) != (1, 3)}
-        pooled[1, 3] = last[:, 0:J]
+        first = [keep.tile([P, J], F32, name=f"first{m}")[:] for m in range(N // P)]
+        second = [keep.tile([P, J], F32, name="second0")[:], early[:, 2 * EARLY_PITCH - LATE_PITCH - H:2 * EARLY_PITCH - LATE_PITCH + H], late[:, H:H + J], keep.tile([P, J], F32, name="second3")[:]]
+        result = {(m, h): keep.tile([P, H], F32, name=f"result{m}_{h}")[:] for m in range(N // P) for h in range(2)}
         acc = {}
 
         def gather_early(i, e0, e1):
-            nc.vector.tensor_tensor(early[:, 2 * J * i + e0:2 * J * i + e1], plane[i][:].indirect(offsets[:, e0 // 16:e1 // 16]),
+            nc.vector.tensor_tensor(early[:, EARLY_PITCH * i + e0:EARLY_PITCH * i + e1], plane[i][:].indirect(offsets[:, e0 // 16:e1 // 16]),
                                     weight_early[:, e0:e1], ALU.mult)
 
         def gather_late(i, j0, j1):
-            nc.vector.tensor_tensor(late[:, 2 * J * i + j0:2 * J * i + j1], plane[i][:].indirect(offsets[:, (2 * J + j0) // 16:(2 * J + j1) // 16]),
+            nc.vector.tensor_tensor(late[:, LATE_PITCH * i + j0:LATE_PITCH * i + j1], plane[i][:].indirect(offsets[:, (2 * J + j0) // 16:(2 * J + j1) // 16]),
                                     weight_late[:, j0:j1], ALU.mult)
 
-        def interleave(c, j0, j1):
-            products = early[:] if c < 2 else late[:]
-            e0 = J * (c % 2) + j0
-            src = products.rearrange("p (i q r) -> p q i r", i=PACK, r=4)[:, e0 // 4:(e0 + j1 - j0) // 4]
-            dst = grouped[c][:, PACK * j0:PACK * j1].rearrange("p (q r i) -> p q i r", i=PACK, r=4)
+        def interleave_pair(c, i0, j0, j1):
+            src = early[:].rearrange("p (i e) -> p e i", i=PACK)[:, J * c + j0:J * c + j1, i0:i0 + 2]
+            dst = grouped[c].rearrange("p (j i) -> p j i", i=PACK)[:, j0:j1, i0:i0 + 2]
             nc.scalar.copy(dst, src)
 
-        def quantize_and_project(c):
-            nc.vector.quantize_mx(out=codes[c][:].bitcast(FP8X4), scales=scales[c][:], in_=grouped[c])
-            for m in range(N // P):
-                acc[c, m] = psum.tile([P, J], F32, name=f"acc{m}")
-                nc.tensor.matmul_mx(out=acc[c, m][:], lhsT=w_codes[:, 2 * P * m:2 * P * (m + 1)].bitcast(FP4X4),
-                                    lhsT_scale=w_scale[:, P * m:P * (m + 1)], rhs=codes[c][:].bitcast(FP8X4),
-                                    rhs_scale=scales[c][:], start=True, stop=True)
+        def interleave_late(j0, j1):
+            src = late.rearrange("p (i q r) -> p q i r", i=PACK, r=4)[:, j0 // 4:j1 // 4]
+            dst = grouped[2][:, PACK * j0:PACK * j1].rearrange("p (q r i) -> p q i r", i=PACK, r=4)
+            nc.scalar.copy(dst, src)
 
-        def pool(c, m, j0=0, j1=J):
-            nc.vector.scalar_tensor_tensor(pooled[c, m][:, j0:j1], acc[c, m][:, j0:j1], bias[:, m:m + 1], pooled[c - 1, m][:, j0:j1], ALU.add, ALU.max)
+        def quantize(c, j0, j1):
+            nc.vector.quantize_mx(out=codes[c][:, j0:j1].bitcast(FP8X4), scales=scales[c][:, j0:j1], in_=grouped[c][:, PACK * j0:PACK * j1])
+
+        def project(dst, c, m, j0, j1):
+            nc.tensor.matmul_mx(out=dst, lhsT=w_codes[:, 2 * P * m:2 * P * (m + 1)].bitcast(FP4X4),
+                                lhsT_scale=w_scale[:, P * m:P * (m + 1)], rhs=codes[c][:, j0:j1].bitcast(FP8X4),
+                                rhs_scale=scales[c][:, j0:j1], start=True, stop=True)
+
+        def project_whole(c, m):
+            acc[c, m] = psum.tile([P, J], F32, name=f"acc{m}")
+            project(acc[c, m][:], c, m, 0, J)
+
+        def project_half(h):
+            for pair in range(2):
+                bank = psum.tile([P, J], F32, name=f"acc{2 * h + pair}")
+                for e in range(2):
+                    m = 2 * pair + e
+                    acc[2, m, h] = bank[:, e * H:(e + 1) * H]
+                    project(acc[2, m, h], 2, m, h * H, (h + 1) * H)
+
+        def pool_first(m):
+            nc.scalar.activation(first[m], acc[1, m][:], ACT.Identity, bias=bias[:, m:m + 1])
+
+        def pool(dst, sums, m, so_far):
+            nc.vector.scalar_tensor_tensor(dst, sums, bias[:, m:m + 1], so_far, ALU.add, ALU.max)
+
+        def pool_second(m):
+            pool(second[m], acc[0, m][:], m, first[m])
+
+        def pool_last_half(m, h, queue):
+            js = slice(h * H, (h + 1) * H)
+            pool(result[m, h], acc[2, m, h], m, second[m][:, js])
+            queue.dma_start(out[P * m:P * (m + 1), js], result[m, h])
 
         gather_early(0, 0, FIRST)
         gather_early(0, FIRST, 2 * J)
         gather_late(0, 0, J)
-        gather_early(1, 0, 2 * J)
+        gather_early(1, J, 2 * J)
+        interleave_pair(1, 0, 0, J)
+        gather_early(1, 0, J)
+        interleave_pair(0, 0, 0, J)
         gather_early(2, 0, 2 * J)
-        gather_early(3, 0, H)
-        interleave(0, 0, H)
-        gather_early(3, H, J)
-        interleave(0, H, J)
-        gather_early(3, J, 2 * J)
-        interleave(1, 0, J)
-        gather_late(1, 0, J)
-        quantize_and_project(0)
+        for j0, j1 in ((0, LEAD), (LEAD, J)):
+            gather_early(3, J + j0, J + j1)
+            interleave_pair(1, 2, j0, j1)
+        gather_early(3, 0, J)
+        interleave_pair(0, 2, 0, J)
+        quantize(1, 0, J)
         for m in range(N // P):
-            nc.scalar.activation(pooled[0, m], acc[0, m][:], ACT.Identity, bias=bias[:, m:m + 1])
+            project_whole(1, m)
+            pool_first(m)
         gather_late(2, 0, J)
-        quantize_and_project(1)
-        gather_late(3, 0, H)
-        interleave(2, 0, H)
-        gather_late(3, H, J)
-        interleave(2, H, J)
-        for m in range(3):
-            pool(1, m)
-        quantize_and_project(2)
-        pool(1, 3)
-        for m in range(3):
-            pool(2, m)
-            nc.sync.dma_start(out[P * m:P * (m + 1), :], pooled[2, m])
-        for h, queue in ((0, nc.scalar), (1, nc.sync)):
-            pool(2, 3, h * H, (h + 1) * H)
-            queue.dma_start(out[3 * P:4 * P, h * H:(h + 1) * H], pooled[2, 3][:, h * H:(h + 1) * H])
+        quantize(0, 0, J)
+        for m in range(N // P):
+            project_whole(0, m)
+        gather_late(1, 0, J)
+        for h in range(2):
+            gather_late(3, h * H, (h + 1) * H)
+            interleave_late(h * H, (h + 1) * H)
+        pool_second(0)
+        quantize(2, 0, H)
+        project_half(0)
+        pool_second(1)
+        pool_last_half(0, 0, nc.sync)
+        quantize(2, H, J)
+        project_half(1)
+        pool_last_half(1, 0, nc.sync)
+        pool_second(2)
+        pool_last_half(0, 1, nc.sync)
+        pool_last_half(2, 0, nc.scalar)
+        pool_second(3)
+        pool_last_half(1, 1, nc.sync)
+        pool_last_half(3, 0, nc.scalar)
+        pool_last_half(2, 1, nc.sync)
+        pool_last_half(3, 1, nc.scalar)

@@ -15,13 +15,21 @@ FP8X4 = mybir.dt.float8_e4m3fn_x4
 FP4X4 = mybir.dt.float4_e2m1fn_x4
 ALU = mybir.AluOpType
 ACT = mybir.ActivationFunctionType
+
 P = 128
 PACK = 4
-H = J // 2
+PER_COLUMN = 16
+N_TILES = N // P
+HALF = J // 2
+LATE = 2
+
 FIRST = 384
+HELD = 192
 LEAD = 192
+
 EARLY_PITCH = 15 * J // 4
 LATE_PITCH = 7 * J // 4
+LATE_START = 2 * EARLY_PITCH - LATE_PITCH
 
 
 def tile_list_max_bias_kernel(tc, xT, wgt, w_words, w_scales, b, offs, out):
@@ -30,13 +38,13 @@ def tile_list_max_bias_kernel(tc, xT, wgt, w_words, w_scales, b, offs, out):
         keep = ctx.enter_context(tc.tile_pool(name="keep", bufs=1))
         psum = ctx.enter_context(tc.psum_pool(name="psum", bufs=2))
 
-        offsets = keep.tile([P, PICKS * J // 16], U16, name="offsets")
+        offsets = keep.tile([P, PICKS * J // PER_COLUMN], U16, name="offsets")
         w_scale = keep.tile([P, N], U8, name="w_scale", align_bytes=64)
         nc.gpsimd.memset(w_scale[:].bitcast(I32), 0)
 
-        early = keep.tile([P, PACK * EARLY_PITCH], F32, name="early")
-        late = early[:, 2 * EARLY_PITCH - LATE_PITCH:2 * EARLY_PITCH + 3 * LATE_PITCH]
-        weight_early = keep.tile([P, 2 * J], F32, name="weight_early")
+        products = keep.tile([P, PACK * EARLY_PITCH], F32, name="products")
+        late_products = products[:, LATE_START:LATE_START + PACK * LATE_PITCH]
+        weight_early = keep.tile([P, LATE * J], F32, name="weight_early")
         weight_late = keep.tile([P, J], F32, name="weight_late")
         grouped = [keep.tile([P, PACK * J], BF16, name=f"grouped{c}", align_bytes=64)[:] for c in range(PICKS)]
 
@@ -45,115 +53,117 @@ def tile_list_max_bias_kernel(tc, xT, wgt, w_words, w_scales, b, offs, out):
         nc.sync.dma_start(plane[0][:], x_planes[:, 0, :])
         nc.sync.dma_start(offsets[:], offs)
         nc.sync.dma_start(weight_early[:, 0:FIRST], wgt[:, 0:FIRST])
-        nc.sync.dma_start(weight_early[:, FIRST:2 * J], wgt[:, FIRST:2 * J])
-        nc.sync.dma_start(weight_late[:], wgt[:, 2 * J:3 * J])
+        nc.sync.dma_start(weight_early[:, FIRST:LATE * J], wgt[:, FIRST:LATE * J])
+        nc.sync.dma_start(weight_late[:, 0:J - HELD], wgt[:, LATE * J:PICKS * J - HELD])
         for i in range(1, PACK):
             nc.sync.dma_start(plane[i][:], x_planes[:, i, :])
+        nc.sync.dma_start(weight_late[:, J - HELD:J], wgt[:, PICKS * J - HELD:PICKS * J])
         w_codes = keep.tile([P, 2 * N], U8, name="w_codes", align_bytes=64)
         nc.sync.dma_start(w_codes[:].bitcast(I32), w_words[0].bitcast(I32))
-        for q in range(4):
-            nc.sync.dma_start(w_scale[32 * q:32 * q + 4, :].bitcast(I32), w_scales[0, 4 * q:4 * q + 4, :].bitcast(I32))
-        bias = keep.tile([P, N // P], F32, name="bias")
+        for quadrant in range(4):
+            nc.sync.dma_start(w_scale[32 * quadrant:32 * quadrant + 4, :].bitcast(I32),
+                              w_scales[0, 4 * quadrant:4 * quadrant + 4, :].bitcast(I32))
+        bias = keep.tile([P, N_TILES], F32, name="bias")
         with nc.allow_non_contiguous_dma(reason="one bias value a partition"):
             nc.sync.dma_start(bias[:], b.rearrange("(m p) -> p m", p=P))
 
         codes = [keep.tile([P, J], U32, name=f"codes{c}", align_bytes=64) for c in range(PICKS)]
         scales = [keep.tile([P, J], U8, name=f"scales{c}", align_bytes=64) for c in range(PICKS)]
-        first = [keep.tile([P, J], F32, name=f"first{m}")[:] for m in range(N // P)]
-        second = [keep.tile([P, J], F32, name="second0")[:], early[:, 2 * EARLY_PITCH - LATE_PITCH - H:2 * EARLY_PITCH - LATE_PITCH + H], late[:, H:H + J], keep.tile([P, J], F32, name="second3")[:]]
-        result = {(m, h): keep.tile([P, H], F32, name=f"result{m}_{h}")[:] for m in range(N // P) for h in range(2)}
-        acc = {}
+        one_pick = [keep.tile([P, J], F32, name=f"one_pick{m}")[:] for m in range(N_TILES)]
+        two_picks = [keep.tile([P, J], F32, name="two_picks0")[:],
+                     products[:, LATE_START - HALF:LATE_START + HALF],
+                     late_products[:, 2 * LATE_PITCH - HALF:2 * LATE_PITCH + HALF],
+                     keep.tile([P, J], F32, name="two_picks3")[:]]
+        result = {(m, h): keep.tile([P, HALF], F32, name=f"result{m}_{h}")[:] for m in range(N_TILES) for h in range(2)}
+        early_sums = {}
+        late_sums = {}
 
         def gather_early(i, e0, e1):
-            nc.vector.tensor_tensor(early[:, EARLY_PITCH * i + e0:EARLY_PITCH * i + e1], plane[i][:].indirect(offsets[:, e0 // 16:e1 // 16]),
+            nc.vector.tensor_tensor(products[:, EARLY_PITCH * i + e0:EARLY_PITCH * i + e1],
+                                    plane[i][:].indirect(offsets[:, e0 // PER_COLUMN:e1 // PER_COLUMN]),
                                     weight_early[:, e0:e1], ALU.mult)
 
         def gather_late(i, j0, j1):
-            nc.vector.tensor_tensor(late[:, LATE_PITCH * i + j0:LATE_PITCH * i + j1], plane[i][:].indirect(offsets[:, (2 * J + j0) // 16:(2 * J + j1) // 16]),
+            e0, e1 = LATE * J + j0, LATE * J + j1
+            nc.vector.tensor_tensor(late_products[:, LATE_PITCH * i + j0:LATE_PITCH * i + j1],
+                                    plane[i][:].indirect(offsets[:, e0 // PER_COLUMN:e1 // PER_COLUMN]),
                                     weight_late[:, j0:j1], ALU.mult)
 
         def interleave_pair(c, i0, j0, j1):
-            src = early[:].rearrange("p (i e) -> p e i", i=PACK)[:, J * c + j0:J * c + j1, i0:i0 + 2]
+            src = products[:].rearrange("p (i e) -> p e i", i=PACK)[:, J * c + j0:J * c + j1, i0:i0 + 2]
             dst = grouped[c].rearrange("p (j i) -> p j i", i=PACK)[:, j0:j1, i0:i0 + 2]
             nc.scalar.copy(dst, src)
 
         def interleave_late(j0, j1):
-            src = late.rearrange("p (i q r) -> p q i r", i=PACK, r=4)[:, j0 // 4:j1 // 4]
-            dst = grouped[2][:, PACK * j0:PACK * j1].rearrange("p (q r i) -> p q i r", i=PACK, r=4)
+            src = late_products.rearrange("p (i q r) -> p q i r", i=PACK, r=4)[:, j0 // 4:j1 // 4]
+            dst = grouped[LATE][:, PACK * j0:PACK * j1].rearrange("p (q r i) -> p q i r", i=PACK, r=4)
             nc.scalar.copy(dst, src)
 
         def quantize(c, j0, j1):
-            nc.vector.quantize_mx(out=codes[c][:, j0:j1].bitcast(FP8X4), scales=scales[c][:, j0:j1], in_=grouped[c][:, PACK * j0:PACK * j1])
+            nc.vector.quantize_mx(out=codes[c][:, j0:j1].bitcast(FP8X4), scales=scales[c][:, j0:j1],
+                                  in_=grouped[c][:, PACK * j0:PACK * j1])
 
-        def project(dst, c, m, j0, j1):
-            nc.tensor.matmul_mx(out=dst, lhsT=w_codes[:, 2 * P * m:2 * P * (m + 1)].bitcast(FP4X4),
+        def project(sums, c, m, j0, j1):
+            nc.tensor.matmul_mx(out=sums, lhsT=w_codes[:, 2 * P * m:2 * P * (m + 1)].bitcast(FP4X4),
                                 lhsT_scale=w_scale[:, P * m:P * (m + 1)], rhs=codes[c][:, j0:j1].bitcast(FP8X4),
                                 rhs_scale=scales[c][:, j0:j1], start=True, stop=True)
 
-        def project_whole(c, m):
-            acc[c, m] = psum.tile([P, J], F32, name=f"acc{m}")
-            project(acc[c, m][:], c, m, 0, J)
+        def project_early(c, m):
+            bank = psum.tile([P, J], F32, name=f"bank{m}")
+            early_sums[c, m] = bank[:]
+            project(early_sums[c, m], c, m, 0, J)
 
-        def project_half(h):
-            for pair in range(2):
-                bank = psum.tile([P, J], F32, name=f"acc{2 * h + pair}")
-                for e in range(2):
-                    m = 2 * pair + e
-                    acc[2, m, h] = bank[:, e * H:(e + 1) * H]
-                    project(acc[2, m, h], 2, m, h * H, (h + 1) * H)
-
-        def pool_first(m):
-            nc.scalar.activation(first[m], acc[1, m][:], ACT.Identity, bias=bias[:, m:m + 1])
+        def project_late(h):
+            for pair in range(N_TILES // 2):
+                bank = psum.tile([P, J], F32, name=f"bank{2 * h + pair}")
+                for side in range(2):
+                    m = 2 * pair + side
+                    late_sums[m, h] = bank[:, side * HALF:(side + 1) * HALF]
+                    project(late_sums[m, h], LATE, m, h * HALF, (h + 1) * HALF)
 
         def pool(dst, sums, m, so_far):
             nc.vector.scalar_tensor_tensor(dst, sums, bias[:, m:m + 1], so_far, ALU.add, ALU.max)
 
-        def pool_second(m):
-            pool(second[m], acc[0, m][:], m, first[m])
-
-        def pool_last_half(m, h, queue):
-            js = slice(h * H, (h + 1) * H)
-            pool(result[m, h], acc[2, m, h], m, second[m][:, js])
-            queue.dma_start(out[P * m:P * (m + 1), js], result[m, h])
+        def pool_early(m):
+            pool(two_picks[m], early_sums[0, m], m, one_pick[m])
 
         gather_early(0, 0, FIRST)
-        gather_early(0, FIRST, 2 * J)
-        gather_late(0, 0, J)
-        gather_early(1, J, 2 * J)
-        interleave_pair(1, 0, 0, J)
-        gather_early(1, 0, J)
-        interleave_pair(0, 0, 0, J)
-        gather_early(2, 0, 2 * J)
+        gather_early(0, FIRST, LATE * J)
+        gather_late(0, 0, J - HELD)
+        for c in (1, 0):
+            gather_early(1, c * J, (c + 1) * J)
+            interleave_pair(c, 0, 0, J)
+        gather_early(2, 0, LATE * J)
+
         for j0, j1 in ((0, LEAD), (LEAD, J)):
             gather_early(3, J + j0, J + j1)
             interleave_pair(1, 2, j0, j1)
         gather_early(3, 0, J)
         interleave_pair(0, 2, 0, J)
+        gather_late(0, J - HELD, J)
+
         quantize(1, 0, J)
-        for m in range(N // P):
-            project_whole(1, m)
-            pool_first(m)
+        for m in range(N_TILES):
+            project_early(1, m)
+            nc.scalar.activation(one_pick[m], early_sums[1, m], ACT.Identity, bias=bias[:, m:m + 1])
         gather_late(2, 0, J)
         quantize(0, 0, J)
-        for m in range(N // P):
-            project_whole(0, m)
+        for m in range(N_TILES):
+            project_early(0, m)
         gather_late(1, 0, J)
         for h in range(2):
-            gather_late(3, h * H, (h + 1) * H)
-            interleave_late(h * H, (h + 1) * H)
-        pool_second(0)
-        quantize(2, 0, H)
-        project_half(0)
-        pool_second(1)
-        pool_last_half(0, 0, nc.sync)
-        quantize(2, H, J)
-        project_half(1)
-        pool_last_half(1, 0, nc.sync)
-        pool_second(2)
-        pool_last_half(0, 1, nc.sync)
-        pool_last_half(2, 0, nc.scalar)
-        pool_second(3)
-        pool_last_half(1, 1, nc.sync)
-        pool_last_half(3, 0, nc.scalar)
-        pool_last_half(2, 1, nc.sync)
-        pool_last_half(3, 1, nc.scalar)
+            gather_late(3, h * HALF, (h + 1) * HALF)
+            interleave_late(h * HALF, (h + 1) * HALF)
+
+        for h, row_tiles in enumerate(((0, 3), (1, 2))):
+            for m in row_tiles:
+                pool_early(m)
+            quantize(LATE, h * HALF, (h + 1) * HALF)
+            project_late(h)
+
+        for h in range(2):
+            places = slice(h * HALF, (h + 1) * HALF)
+            for m in range(N_TILES):
+                pool(result[m, h], late_sums[m, h], m, two_picks[m][:, places])
+                queue = nc.sync if m % 2 == 0 else nc.scalar
+                queue.dma_start(out[P * m:P * (m + 1), places], result[m, h])

@@ -23,7 +23,7 @@ N_TILES = N // P
 HALF = J // 2
 LATE = 2
 
-FIRST = 384
+BLOCK = 32
 HELD = 192
 LEAD = 192
 
@@ -44,16 +44,18 @@ def tile_list_max_bias_kernel(tc, xT, wgt, w_words, w_scales, b, offs, out):
 
         products = keep.tile([P, PACK * EARLY_PITCH], F32, name="products")
         late_products = products[:, LATE_START:LATE_START + PACK * LATE_PITCH]
-        weight_early = keep.tile([P, LATE * J], F32, name="weight_early")
+        weight_early = keep.tile([P, LATE * J], F32, name="weight_early", align_bytes=64)
         weight_late = keep.tile([P, J], F32, name="weight_late")
         grouped = [keep.tile([P, PACK * J], BF16, name=f"grouped{c}", align_bytes=64)[:] for c in range(PICKS)]
 
         x_planes = xT.rearrange("(p i) t -> p i t", i=PACK)
         plane = [keep.tile([P, T], F32, name=f"plane{i}") for i in range(PACK)]
+        dealt = keep.tile([P, LATE * BLOCK], F32, name="dealt", align_bytes=64)
+        turned = keep.tile([P, LATE * BLOCK], F32, name="turned", align_bytes=64)
+        spread = [keep.tile([P, J], F32, name=f"spread{c}", align_bytes=64) for c in range(LATE)]
+        nc.sync.dma_start(dealt[:], wgt[0:P:PER_COLUMN, 0:LATE * J].rearrange("g (r e) -> g r e", r=PER_COLUMN))
         nc.sync.dma_start(plane[0][:], x_planes[:, 0, :])
         nc.sync.dma_start(offsets[:], offs)
-        nc.sync.dma_start(weight_early[:, 0:FIRST], wgt[:, 0:FIRST])
-        nc.sync.dma_start(weight_early[:, FIRST:LATE * J], wgt[:, FIRST:LATE * J])
         nc.sync.dma_start(weight_late[:, 0:J - HELD], wgt[:, LATE * J:PICKS * J - HELD])
         for i in range(1, PACK):
             nc.sync.dma_start(plane[i][:], x_planes[:, i, :])
@@ -66,6 +68,15 @@ def tile_list_max_bias_kernel(tc, xT, wgt, w_words, w_scales, b, offs, out):
         bias = keep.tile([P, N_TILES], F32, name="bias")
         with nc.allow_non_contiguous_dma(reason="one bias value a partition"):
             nc.sync.dma_start(bias[:], b.rearrange("(m p) -> p m", p=P))
+
+        for u in range(LATE):
+            nc.vector.transpose(turned[:, u * BLOCK:(u + 1) * BLOCK], dealt[:, u * BLOCK:(u + 1) * BLOCK])
+        runs = PER_COLUMN // LATE
+        for c, copy in enumerate((nc.vector.tensor_copy, nc.scalar.copy)):
+            src = turned[:].rearrange("p (u h r) -> p r u h", u=LATE, h=2)[:, c * runs:(c + 1) * runs]
+            copy(spread[c][:].rearrange("p (r u h s) -> p r u h s", u=LATE, h=2, s=PER_COLUMN),
+                 src.unsqueeze(4).to_broadcast([P, runs, LATE, 2, PER_COLUMN]))
+            nc.vector.transpose(weight_early[:, c * J:(c + 1) * J], spread[c][:])
 
         codes = [keep.tile([P, J], U32, name=f"codes{c}", align_bytes=64) for c in range(PICKS)]
         scales = [keep.tile([P, J], U8, name=f"scales{c}", align_bytes=64) for c in range(PICKS)]
@@ -127,8 +138,7 @@ def tile_list_max_bias_kernel(tc, xT, wgt, w_words, w_scales, b, offs, out):
         def pool_early(m):
             pool(two_picks[m], early_sums[0, m], m, one_pick[m])
 
-        gather_early(0, 0, FIRST)
-        gather_early(0, FIRST, LATE * J)
+        gather_early(0, 0, LATE * J)
         gather_late(0, 0, J - HELD)
         for c in (1, 0):
             gather_early(1, c * J, (c + 1) * J)

@@ -18,48 +18,43 @@ ACT = mybir.ActivationFunctionType
 
 P = 128
 PACK = 4
-PER_COLUMN = 16
+GROUP = 16
+BLOCK = 32
 N_TILES = N // P
 HALF = J // 2
 LATE = 2
-
-BLOCK = 32
-HELD = 192
-LEAD = 192
-
-EARLY_PITCH = 15 * J // 4
-LATE_PITCH = 7 * J // 4
-LATE_START = 2 * EARLY_PITCH - LATE_PITCH
+EARLY = LATE * J
+LATE_ON = ((0, 1), (1, 1), (2, 1), (3, 0))
 
 
 def tile_list_max_bias_kernel(tc, xT, wgt, w_words, w_scales, b, offs, out):
     nc = tc.nc
     with ExitStack() as ctx:
         keep = ctx.enter_context(tc.tile_pool(name="keep", bufs=1))
-        psum = ctx.enter_context(tc.psum_pool(name="psum", bufs=2))
+        psum = ctx.enter_context(tc.psum_pool(name="psum", bufs=1))
 
-        offsets = keep.tile([P, PICKS * J // PER_COLUMN], U16, name="offsets")
+        offsets = keep.tile([P, PICKS * J // GROUP], U16, name="offsets")
         w_scale = keep.tile([P, N], U8, name="w_scale", align_bytes=64)
         nc.gpsimd.memset(w_scale[:].bitcast(I32), 0)
 
-        products = keep.tile([P, PACK * EARLY_PITCH], F32, name="products")
-        late_products = products[:, LATE_START:LATE_START + PACK * LATE_PITCH]
-        weight_early = keep.tile([P, LATE * J], F32, name="weight_early", align_bytes=64)
-        weight_late = keep.tile([P, J], F32, name="weight_late")
+        products = keep.tile([P, (PACK + 1) * EARLY], F32, name="products")
+        weight_early = keep.tile([P, EARLY], F32, name="weight_early", align_bytes=64)
+        late_room = keep.tile([P, 2 * J], F32, name="late_room")
+        weight_late = late_room[:, HALF:HALF + J]
         grouped = [keep.tile([P, PACK * J], BF16, name=f"grouped{c}", align_bytes=64)[:] for c in range(PICKS)]
 
-        x_planes = xT.rearrange("(p i) t -> p i t", i=PACK)
-        plane = [keep.tile([P, T], F32, name=f"plane{i}") for i in range(PACK)]
         dealt = keep.tile([P, LATE * BLOCK], F32, name="dealt", align_bytes=64)
         turned = keep.tile([P, LATE * BLOCK], F32, name="turned", align_bytes=64)
         spread = [keep.tile([P, J], F32, name=f"spread{c}", align_bytes=64) for c in range(LATE)]
-        nc.sync.dma_start(dealt[:], wgt[0:P:PER_COLUMN, 0:LATE * J].rearrange("g (r e) -> g r e", r=PER_COLUMN))
+        nc.sync.dma_start(dealt[:], wgt[0:P:GROUP, 0:EARLY].rearrange("g (r e) -> g r e", r=GROUP))
+
+        x_planes = xT.rearrange("(p i) t -> p i t", i=PACK)
+        plane = [keep.tile([P, T], F32, name=f"plane{i}") for i in range(PACK)]
         nc.sync.dma_start(plane[0][:], x_planes[:, 0, :])
         nc.sync.dma_start(offsets[:], offs)
-        nc.sync.dma_start(weight_late[:, 0:J - HELD], wgt[:, LATE * J:PICKS * J - HELD])
         for i in range(1, PACK):
             nc.sync.dma_start(plane[i][:], x_planes[:, i, :])
-        nc.sync.dma_start(weight_late[:, J - HELD:J], wgt[:, PICKS * J - HELD:PICKS * J])
+        nc.sync.dma_start(weight_late, wgt[:, EARLY:PICKS * J])
         w_codes = keep.tile([P, 2 * N], U8, name="w_codes", align_bytes=64)
         nc.sync.dma_start(w_codes[:].bitcast(I32), w_words[0].bitcast(I32))
         for quadrant in range(4):
@@ -71,109 +66,117 @@ def tile_list_max_bias_kernel(tc, xT, wgt, w_words, w_scales, b, offs, out):
 
         for u in range(LATE):
             nc.vector.transpose(turned[:, u * BLOCK:(u + 1) * BLOCK], dealt[:, u * BLOCK:(u + 1) * BLOCK])
-        runs = PER_COLUMN // LATE
+        runs = GROUP // LATE
         for c, copy in enumerate((nc.vector.tensor_copy, nc.scalar.copy)):
             src = turned[:].rearrange("p (u h r) -> p r u h", u=LATE, h=2)[:, c * runs:(c + 1) * runs]
-            copy(spread[c][:].rearrange("p (r u h s) -> p r u h s", u=LATE, h=2, s=PER_COLUMN),
-                 src.unsqueeze(4).to_broadcast([P, runs, LATE, 2, PER_COLUMN]))
+            copy(spread[c][:].rearrange("p (r u h s) -> p r u h s", u=LATE, h=2, s=GROUP),
+                 src.unsqueeze(4).to_broadcast([P, runs, LATE, 2, GROUP]))
             nc.vector.transpose(weight_early[:, c * J:(c + 1) * J], spread[c][:])
+
+        def column(i, c):
+            if c == LATE:
+                i, c = LATE_ON[i]
+            return i * EARLY + c * J
 
         codes = [keep.tile([P, J], U32, name=f"codes{c}", align_bytes=64) for c in range(PICKS)]
         scales = [keep.tile([P, J], U8, name=f"scales{c}", align_bytes=64) for c in range(PICKS)]
-        one_pick = [keep.tile([P, J], F32, name=f"one_pick{m}")[:] for m in range(N_TILES)]
-        two_picks = [keep.tile([P, J], F32, name="two_picks0")[:],
-                     products[:, LATE_START - HALF:LATE_START + HALF],
-                     late_products[:, 2 * LATE_PITCH - HALF:2 * LATE_PITCH + HALF],
-                     keep.tile([P, J], F32, name="two_picks3")[:]]
-        result = {(m, h): keep.tile([P, HALF], F32, name=f"result{m}_{h}")[:] for m in range(N_TILES) for h in range(2)}
-        early_sums = {}
-        late_sums = {}
+        one_pick = [keep.tile([P, J], F32, name=f"one_pick{m}")[:] for m in range(2)]
+        one_pick.extend(late_room[:, h * J:(h + 1) * J] for h in range(2))
+        two_picks = [products[:, column(2, LATE) - HALF:column(2, LATE) + HALF] if m == 1
+                     else keep.tile([P, J], F32, name=f"two_picks{m}")[:] for m in range(N_TILES)]
+        result = [keep.tile([P, J], F32, name=f"result{m}")[:] for m in range(N_TILES)]
+        sums = {}
 
-        def gather_early(i, e0, e1):
-            nc.vector.tensor_tensor(products[:, EARLY_PITCH * i + e0:EARLY_PITCH * i + e1],
-                                    plane[i][:].indirect(offsets[:, e0 // PER_COLUMN:e1 // PER_COLUMN]),
-                                    weight_early[:, e0:e1], ALU.mult)
+        def gather(i, c, j0, j1):
+            weight = weight_late if c == LATE else weight_early[:, c * J:EARLY]
+            e0, e1 = c * J + j0, c * J + j1
+            nc.vector.tensor_tensor(products[:, column(i, c) + j0:column(i, c) + j1],
+                                    plane[i][:].indirect(offsets[:, e0 // GROUP:e1 // GROUP]),
+                                    weight[:, j0:j1], ALU.mult)
 
-        def gather_late(i, j0, j1):
-            e0, e1 = LATE * J + j0, LATE * J + j1
-            nc.vector.tensor_tensor(late_products[:, LATE_PITCH * i + j0:LATE_PITCH * i + j1],
-                                    plane[i][:].indirect(offsets[:, e0 // PER_COLUMN:e1 // PER_COLUMN]),
-                                    weight_late[:, j0:j1], ALU.mult)
-
-        def interleave_pair(c, i0, j0, j1):
-            src = products[:].rearrange("p (i e) -> p e i", i=PACK)[:, J * c + j0:J * c + j1, i0:i0 + 2]
+        def interleave(c, i0, j0, j1):
+            first = column(i0, c)
+            pitch = column(i0 + 1, c) - first
+            src = products[:, first:first + 2 * pitch].rearrange("p (i e) -> p e i", i=2)[:, j0:j1, :]
             dst = grouped[c].rearrange("p (j i) -> p j i", i=PACK)[:, j0:j1, i0:i0 + 2]
-            nc.scalar.copy(dst, src)
-
-        def interleave_late(j0, j1):
-            src = late_products.rearrange("p (i q r) -> p q i r", i=PACK, r=4)[:, j0 // 4:j1 // 4]
-            dst = grouped[LATE][:, PACK * j0:PACK * j1].rearrange("p (q r i) -> p q i r", i=PACK, r=4)
             nc.scalar.copy(dst, src)
 
         def quantize(c, j0, j1):
             nc.vector.quantize_mx(out=codes[c][:, j0:j1].bitcast(FP8X4), scales=scales[c][:, j0:j1],
                                   in_=grouped[c][:, PACK * j0:PACK * j1])
 
-        def project(sums, c, m, j0, j1):
-            nc.tensor.matmul_mx(out=sums, lhsT=w_codes[:, 2 * P * m:2 * P * (m + 1)].bitcast(FP4X4),
+        def project(dst, c, m, j0, j1):
+            nc.tensor.matmul_mx(out=dst, lhsT=w_codes[:, 2 * P * m:2 * P * (m + 1)].bitcast(FP4X4),
                                 lhsT_scale=w_scale[:, P * m:P * (m + 1)], rhs=codes[c][:, j0:j1].bitcast(FP8X4),
                                 rhs_scale=scales[c][:, j0:j1], start=True, stop=True)
 
-        def project_early(c, m):
-            bank = psum.tile([P, J], F32, name=f"bank{m}")
-            early_sums[c, m] = bank[:]
-            project(early_sums[c, m], c, m, 0, J)
+        def project_early(c, m, bank):
+            sums[c, m] = psum.tile([P, J], F32, name=f"bank{bank}")[:]
+            project(sums[c, m], c, m, 0, J)
 
-        def project_late(h):
-            for pair in range(N_TILES // 2):
-                bank = psum.tile([P, J], F32, name=f"bank{2 * h + pair}")
-                for side in range(2):
-                    m = 2 * pair + side
-                    late_sums[m, h] = bank[:, side * HALF:(side + 1) * HALF]
-                    project(late_sums[m, h], LATE, m, h * HALF, (h + 1) * HALF)
+        def move_first(m):
+            nc.scalar.activation(one_pick[m], sums[1, m], ACT.Identity, bias=bias[:, m:m + 1])
 
-        def pool(dst, sums, m, so_far):
-            nc.vector.scalar_tensor_tensor(dst, sums, bias[:, m:m + 1], so_far, ALU.add, ALU.max)
+        def pool(dst, src, m, so_far):
+            nc.vector.scalar_tensor_tensor(dst, src, bias[:, m:m + 1], so_far, ALU.add, ALU.max)
 
         def pool_early(m):
-            pool(two_picks[m], early_sums[0, m], m, one_pick[m])
+            pool(two_picks[m], sums[0, m], m, one_pick[m])
 
-        gather_early(0, 0, LATE * J)
-        gather_late(0, 0, J - HELD)
+        def finish(dst, src, m, j0, j1, queue):
+            pool(dst, src, m, two_picks[m][:, j0:j1])
+            queue.dma_start(out[P * m:P * (m + 1), j0:j1], dst)
+
+        gather(0, 0, 0, EARLY)
+        gather(1, 0, 0, EARLY)
         for c in (1, 0):
-            gather_early(1, c * J, (c + 1) * J)
-            interleave_pair(c, 0, 0, J)
-        gather_early(2, 0, LATE * J)
-
-        for j0, j1 in ((0, LEAD), (LEAD, J)):
-            gather_early(3, J + j0, J + j1)
-            interleave_pair(1, 2, j0, j1)
-        gather_early(3, 0, J)
-        interleave_pair(0, 2, 0, J)
-        gather_late(0, J - HELD, J)
-
+            interleave(c, 0, 0, J)
+        gather(2, 0, 0, EARLY)
+        for c in (1, 0):
+            gather(3, c, 0, J)
+            interleave(c, 2, 0, J)
+        for i in range(2):
+            gather(i, LATE, 0, J)
+        interleave(LATE, 0, 0, J)
         quantize(1, 0, J)
-        for m in range(N_TILES):
-            project_early(1, m)
-            nc.scalar.activation(one_pick[m], early_sums[1, m], ACT.Identity, bias=bias[:, m:m + 1])
-        gather_late(2, 0, J)
+        for m in range(3):
+            project_early(1, m, m)
+        gather(2, LATE, 0, J)
         quantize(0, 0, J)
         for m in range(N_TILES):
-            project_early(0, m)
-        gather_late(1, 0, J)
+            project_early(0, m, N_TILES + m)
+        for m in range(2):
+            move_first(m)
         for h in range(2):
-            gather_late(3, h * HALF, (h + 1) * HALF)
-            interleave_late(h * HALF, (h + 1) * HALF)
+            gather(3, LATE, h * HALF, (h + 1) * HALF)
+            interleave(LATE, 2, h * HALF, (h + 1) * HALF)
+        move_first(2)
 
-        for h, row_tiles in enumerate(((0, 3), (1, 2))):
-            for m in row_tiles:
-                pool_early(m)
-            quantize(LATE, h * HALF, (h + 1) * HALF)
-            project_late(h)
-
-        for h in range(2):
-            places = slice(h * HALF, (h + 1) * HALF)
-            for m in range(N_TILES):
-                pool(result[m, h], late_sums[m, h], m, two_picks[m][:, places])
-                queue = nc.sync if m % 2 == 0 else nc.scalar
-                queue.dma_start(out[P * m:P * (m + 1), places], result[m, h])
+        pool_early(0)
+        project_early(1, 3, N_TILES)
+        move_first(3)
+        quantize(LATE, 0, HALF)
+        first_halves = psum.tile([P, J], F32, name="bank0")
+        for m in range(2):
+            project(first_halves[:, m * HALF:(m + 1) * HALF], LATE, m, 0, HALF)
+        tile2 = psum.tile([P, J], F32, name="bank1")
+        pool_early(1)
+        quantize(LATE, HALF, J)
+        second_halves = psum.tile([P, J], F32, name="bank2")
+        for m in range(2):
+            project(second_halves[:, m * HALF:(m + 1) * HALF], LATE, m, HALF, J)
+        project(tile2[:], LATE, 2, 0, J)
+        tile3 = psum.tile([P, J], F32, name="bank4")
+        project(tile3[:], LATE, 3, 0, J)
+        for m in range(2):
+            start = column(2 + m, LATE) + HALF
+            finish(products[:, start:start + HALF], first_halves[:, m * HALF:(m + 1) * HALF], m, 0, HALF,
+                   nc.sync)
+        pool_early(2)
+        finish(result[0][:, HALF:J], second_halves[:, 0:HALF], 0, HALF, J, nc.sync)
+        pool_early(3)
+        finish(result[1][:, HALF:J], second_halves[:, HALF:J], 1, HALF, J, nc.scalar)
+        for m, bank in ((2, tile2), (3, tile3)):
+            for h, queue in enumerate((nc.sync, nc.scalar)):
+                places = slice(h * HALF, (h + 1) * HALF)
+                finish(result[m][:, places], bank[:, places], m, places.start, places.stop, queue)

@@ -24,7 +24,6 @@ N_TILES = N // P
 HALF = J // 2
 LATE = 2
 EARLY = LATE * J
-LATE_ON = ((0, 1), (1, 1), (2, 1), (3, 0))
 
 
 def tile_list_max_bias_kernel(tc, xT, wgt, w_words, w_scales, b, offs, out):
@@ -39,8 +38,8 @@ def tile_list_max_bias_kernel(tc, xT, wgt, w_words, w_scales, b, offs, out):
 
         products = keep.tile([P, (PACK + 1) * EARLY], F32, name="products")
         weight_early = keep.tile([P, EARLY], F32, name="weight_early", align_bytes=64)
-        late_room = keep.tile([P, 2 * J], F32, name="late_room")
-        weight_late = late_room[:, HALF:HALF + J]
+        late_room = keep.tile([P, J + HALF], F32, name="late_room")
+        weight_late = late_room[:, 0:J]
         grouped = [keep.tile([P, PACK * J], BF16, name=f"grouped{c}", align_bytes=64)[:] for c in range(PICKS)]
 
         dealt = keep.tile([P, LATE * BLOCK], F32, name="dealt", align_bytes=64)
@@ -73,31 +72,29 @@ def tile_list_max_bias_kernel(tc, xT, wgt, w_words, w_scales, b, offs, out):
                  src.unsqueeze(4).to_broadcast([P, runs, LATE, 2, GROUP]))
             nc.vector.transpose(weight_early[:, c * J:(c + 1) * J], spread[c][:])
 
-        def column(i, c):
+        def column(i, c, j):
             if c == LATE:
-                i, c = LATE_ON[i]
-            return i * EARLY + c * J
+                c, j = (1, j) if i < 2 else (1 - j // HALF, j % HALF)
+            return i * EARLY + c * J + j
 
         codes = [keep.tile([P, J], U32, name=f"codes{c}", align_bytes=64) for c in range(PICKS)]
         scales = [keep.tile([P, J], U8, name=f"scales{c}", align_bytes=64) for c in range(PICKS)]
-        one_pick = [keep.tile([P, J], F32, name=f"one_pick{m}")[:] for m in range(2)]
-        one_pick.extend(late_room[:, h * J:(h + 1) * J] for h in range(2))
-        two_picks = [products[:, column(2, LATE) - HALF:column(2, LATE) + HALF] if m == 1
-                     else keep.tile([P, J], F32, name=f"two_picks{m}")[:] for m in range(N_TILES)]
+        one_pick = [late_room[:, HALF:HALF + J] if m == 2 else keep.tile([P, J], F32, name=f"one_pick{m}")[:]
+                    for m in range(N_TILES)]
+        two_picks = [keep.tile([P, J], F32, name=f"two_picks{m}")[:] for m in range(N_TILES)]
         result = [keep.tile([P, J], F32, name=f"result{m}")[:] for m in range(N_TILES)]
         sums = {}
 
         def gather(i, c, j0, j1):
             weight = weight_late if c == LATE else weight_early[:, c * J:EARLY]
             e0, e1 = c * J + j0, c * J + j1
-            nc.vector.tensor_tensor(products[:, column(i, c) + j0:column(i, c) + j1],
+            nc.vector.tensor_tensor(products[:, column(i, c, j0):column(i, c, j0) + j1 - j0],
                                     plane[i][:].indirect(offsets[:, e0 // GROUP:e1 // GROUP]),
                                     weight[:, j0:j1], ALU.mult)
 
         def interleave(c, i0, j0, j1):
-            first = column(i0, c)
-            pitch = column(i0 + 1, c) - first
-            src = products[:, first:first + 2 * pitch].rearrange("p (i e) -> p e i", i=2)[:, j0:j1, :]
+            first = column(i0, c, j0)
+            src = products[:, first:first + 2 * EARLY].rearrange("p (i e) -> p e i", i=2)[:, 0:j1 - j0, :]
             dst = grouped[c].rearrange("p (j i) -> p j i", i=PACK)[:, j0:j1, i0:i0 + 2]
             nc.scalar.copy(dst, src)
 
@@ -141,25 +138,27 @@ def tile_list_max_bias_kernel(tc, xT, wgt, w_words, w_scales, b, offs, out):
         quantize(1, 0, J)
         for m in range(3):
             project_early(1, m, m)
-        gather(2, LATE, 0, J)
+        for i in (2, 3):
+            gather(i, LATE, 0, HALF)
+        move_first(0)
+        interleave(LATE, 2, 0, HALF)
         quantize(0, 0, J)
         for m in range(N_TILES):
             project_early(0, m, N_TILES + m)
-        for m in range(2):
-            move_first(m)
-        for h in range(2):
-            gather(3, LATE, h * HALF, (h + 1) * HALF)
-            interleave(LATE, 2, h * HALF, (h + 1) * HALF)
+        for i in (2, 3):
+            gather(i, LATE, HALF, J)
+        move_first(1)
+        interleave(LATE, 2, HALF, J)
         move_first(2)
 
-        pool_early(0)
-        project_early(1, 3, N_TILES)
-        move_first(3)
         quantize(LATE, 0, HALF)
         first_halves = psum.tile([P, J], F32, name="bank0")
         for m in range(2):
             project(first_halves[:, m * HALF:(m + 1) * HALF], LATE, m, 0, HALF)
         tile2 = psum.tile([P, J], F32, name="bank1")
+        pool_early(0)
+        project_early(1, 3, N_TILES)
+        move_first(3)
         pool_early(1)
         quantize(LATE, HALF, J)
         second_halves = psum.tile([P, J], F32, name="bank2")
@@ -169,7 +168,7 @@ def tile_list_max_bias_kernel(tc, xT, wgt, w_words, w_scales, b, offs, out):
         tile3 = psum.tile([P, J], F32, name="bank4")
         project(tile3[:], LATE, 3, 0, J)
         for m in range(2):
-            start = column(2 + m, LATE) + HALF
+            start = column(2 + m, LATE, HALF)
             finish(products[:, start:start + HALF], first_halves[:, m * HALF:(m + 1) * HALF], m, 0, HALF,
                    nc.sync)
         pool_early(2)

@@ -81,7 +81,7 @@ def tile_list_max_bias_kernel(tc, xT, wgt, w_words, w_scales, b, offs, out):
         scales = [keep.tile([P, J], U8, name=f"scales{c}", align_bytes=64) for c in range(PICKS)]
         one_pick = [late_room[:, HALF:HALF + J] if m == 2 else keep.tile([P, J], F32, name=f"one_pick{m}")[:]
                     for m in range(N_TILES)]
-        two_picks = [keep.tile([P, J], F32, name=f"two_picks{m}")[:] for m in range(N_TILES)]
+        two_picks = [keep.tile([P, J], F32, name=f"two_picks{m}")[:] for m in range(N_TILES - 1)]
         result = [keep.tile([P, J], F32, name=f"result{m}")[:] for m in range(N_TILES)]
         sums = {}
 
@@ -120,9 +120,9 @@ def tile_list_max_bias_kernel(tc, xT, wgt, w_words, w_scales, b, offs, out):
         def pool_early(m):
             pool(two_picks[m], sums[0, m], m, one_pick[m])
 
-        def finish(dst, src, m, j0, j1, queue):
-            pool(dst, src, m, two_picks[m][:, j0:j1])
-            queue.dma_start(out[P * m:P * (m + 1), j0:j1], dst)
+        def finish(dst, src, so_far, m, j0, queue):
+            pool(dst, src, m, so_far)
+            queue.dma_start(out[P * m:P * (m + 1), j0:j0 + HALF], dst)
 
         gather(0, 0, 0, EARLY)
         gather(1, 0, 0, EARLY)
@@ -169,13 +169,15 @@ def tile_list_max_bias_kernel(tc, xT, wgt, w_words, w_scales, b, offs, out):
         project(tile3[:], LATE, 3, 0, J)
         for m in range(2):
             start = column(2 + m, LATE, HALF)
-            finish(products[:, start:start + HALF], first_halves[:, m * HALF:(m + 1) * HALF], m, 0, HALF,
-                   nc.sync)
+            finish(products[:, start:start + HALF], first_halves[:, m * HALF:(m + 1) * HALF],
+                   two_picks[m][:, 0:HALF], m, 0, nc.sync)
         pool_early(2)
-        finish(result[0][:, HALF:J], second_halves[:, 0:HALF], 0, HALF, J, nc.sync)
-        pool_early(3)
-        finish(result[1][:, HALF:J], second_halves[:, HALF:J], 1, HALF, J, nc.scalar)
-        for m, bank in ((2, tile2), (3, tile3)):
-            for h, queue in enumerate((nc.sync, nc.scalar)):
-                places = slice(h * HALF, (h + 1) * HALF)
-                finish(result[m][:, places], bank[:, places], m, places.start, places.stop, queue)
+        halves = [slice(h * HALF, (h + 1) * HALF) for h in range(2)]
+        for m, queue in enumerate((nc.sync, nc.scalar)):
+            finish(result[m][:, HALF:J], second_halves[:, halves[m]], two_picks[m][:, HALF:J], m, HALF, queue)
+        finish(result[2][:, 0:HALF], tile2[:, 0:HALF], two_picks[2][:, 0:HALF], 2, 0, nc.sync)
+        for h in range(2):
+            pool(two_picks[h][:, HALF:J], sums[0, 3][:, halves[h]], 3, one_pick[3][:, halves[h]])
+        finish(result[2][:, HALF:J], tile2[:, HALF:J], two_picks[2][:, HALF:J], 2, HALF, nc.scalar)
+        for h, queue in enumerate((nc.sync, nc.scalar)):
+            finish(result[3][:, halves[h]], tile3[:, halves[h]], two_picks[h][:, HALF:J], 3, h * HALF, queue)

@@ -81,7 +81,7 @@ def tile_list_max_bias_kernel(tc, xT, wgt, w_words, w_scales, b, offs, out):
         scales = [keep.tile([P, J], U8, name=f"scales{c}", align_bytes=64) for c in range(PICKS)]
         one_pick = [late_room[:, HALF:HALF + J] if m == 2 else keep.tile([P, J], F32, name=f"one_pick{m}")[:]
                     for m in range(N_TILES)]
-        two_picks = [keep.tile([P, J], F32, name=f"two_picks{m}")[:] for m in range(N_TILES - 1)]
+        two_picks = [keep.tile([P, J], F32, name=f"two_picks{m}")[:] for m in range(N_TILES)]
         result = [keep.tile([P, J], F32, name=f"result{m}")[:] for m in range(N_TILES)]
         sums = {}
 
@@ -96,23 +96,23 @@ def tile_list_max_bias_kernel(tc, xT, wgt, w_words, w_scales, b, offs, out):
             first = column(i0, c, j0)
             src = products[:, first:first + 2 * EARLY].rearrange("p (i e) -> p e i", i=2)[:, 0:j1 - j0, :]
             dst = grouped[c].rearrange("p (j i) -> p j i", i=PACK)[:, j0:j1, i0:i0 + 2]
-            nc.scalar.copy(dst, src)
+            nc.scalar.activation(dst, src, ACT.Copy, scale=-1.0 if c == 1 else 1.0)
 
         def quantize(c, j0, j1):
             nc.vector.quantize_mx(out=codes[c][:, j0:j1].bitcast(FP8X4), scales=scales[c][:, j0:j1],
                                   in_=grouped[c][:, PACK * j0:PACK * j1])
 
-        def project(dst, c, m, j0, j1):
+        def project(dst, c, m, j0, j1, start=True, stop=True):
             nc.tensor.matmul_mx(out=dst, lhsT=w_codes[:, 2 * P * m:2 * P * (m + 1)].bitcast(FP4X4),
                                 lhsT_scale=w_scale[:, P * m:P * (m + 1)], rhs=codes[c][:, j0:j1].bitcast(FP8X4),
-                                rhs_scale=scales[c][:, j0:j1], start=True, stop=True)
+                                rhs_scale=scales[c][:, j0:j1], start=start, stop=stop)
 
         def project_early(c, m, bank):
             sums[c, m] = psum.tile([P, J], F32, name=f"bank{bank}")[:]
             project(sums[c, m], c, m, 0, J)
 
         def move_first(m):
-            nc.scalar.activation(one_pick[m], sums[1, m], ACT.Identity, bias=bias[:, m:m + 1])
+            nc.scalar.activation(one_pick[m], sums[1, m], ACT.Identity, bias=bias[:, m:m + 1], scale=-1.0)
 
         def pool(dst, src, m, so_far):
             nc.vector.scalar_tensor_tensor(dst, src, bias[:, m:m + 1], so_far, ALU.add, ALU.max)
@@ -143,11 +143,14 @@ def tile_list_max_bias_kernel(tc, xT, wgt, w_words, w_scales, b, offs, out):
         move_first(0)
         interleave(LATE, 2, 0, HALF)
         quantize(0, 0, J)
-        for m in range(N_TILES):
+        for m in range(N_TILES - 1):
             project_early(0, m, N_TILES + m)
         for i in (2, 3):
             gather(i, LATE, HALF, J)
         move_first(1)
+        lead = psum.tile([P, J], F32, name="bank1")
+        project(lead[:], 0, 3, 0, J, stop=False)
+        project(lead[:], 1, 3, 0, J, start=False)
         interleave(LATE, 2, HALF, J)
         move_first(2)
 
@@ -155,12 +158,18 @@ def tile_list_max_bias_kernel(tc, xT, wgt, w_words, w_scales, b, offs, out):
         first_halves = psum.tile([P, J], F32, name="bank0")
         for m in range(2):
             project(first_halves[:, m * HALF:(m + 1) * HALF], LATE, m, 0, HALF)
-        tile2 = psum.tile([P, J], F32, name="bank1")
+        tile2 = psum.tile([P, J], F32, name="bank7")
         pool_early(0)
         project_early(1, 3, N_TILES)
-        move_first(3)
+        gain = [keep.tile([P, HALF], F32, name="gain")[:], grouped[LATE][:, PACK * HALF:PACK * HALF + J].bitcast(F32)]
+        halves = [slice(h * HALF, (h + 1) * HALF) for h in range(2)]
         pool_early(1)
         quantize(LATE, HALF, J)
+        for h, places in enumerate(halves):
+            nc.scalar.activation(gain[h], lead[:, places], ACT.Relu)
+            nc.scalar.activation(one_pick[3][:, places], sums[1, 3][:, places], ACT.Identity, bias=bias[:, 3:4],
+                                 scale=-1.0)
+            nc.gpsimd.tensor_tensor(two_picks[3][:, places], gain[h], one_pick[3][:, places], ALU.add)
         second_halves = psum.tile([P, J], F32, name="bank2")
         for m in range(2):
             project(second_halves[:, m * HALF:(m + 1) * HALF], LATE, m, HALF, J)
@@ -171,13 +180,12 @@ def tile_list_max_bias_kernel(tc, xT, wgt, w_words, w_scales, b, offs, out):
             start = column(2 + m, LATE, HALF)
             finish(products[:, start:start + HALF], first_halves[:, m * HALF:(m + 1) * HALF],
                    two_picks[m][:, 0:HALF], m, 0, nc.sync)
-        pool_early(2)
-        halves = [slice(h * HALF, (h + 1) * HALF) for h in range(2)]
+        third = (two_picks[2][:, 0:HALF], two_picks[0][:, HALF:J])
+        pool(third[0], sums[0, 2][:, 0:HALF], 2, one_pick[2][:, 0:HALF])
         for m, queue in enumerate((nc.sync, nc.scalar)):
             finish(result[m][:, HALF:J], second_halves[:, halves[m]], two_picks[m][:, HALF:J], m, HALF, queue)
-        finish(result[2][:, 0:HALF], tile2[:, 0:HALF], two_picks[2][:, 0:HALF], 2, 0, nc.sync)
-        for h in range(2):
-            pool(two_picks[h][:, HALF:J], sums[0, 3][:, halves[h]], 3, one_pick[3][:, halves[h]])
-        finish(result[2][:, HALF:J], tile2[:, HALF:J], two_picks[2][:, HALF:J], 2, HALF, nc.scalar)
-        for h, queue in enumerate((nc.sync, nc.scalar)):
-            finish(result[3][:, halves[h]], tile3[:, halves[h]], two_picks[h][:, HALF:J], 3, h * HALF, queue)
+        finish(result[2][:, 0:HALF], tile2[:, 0:HALF], third[0], 2, 0, nc.sync)
+        pool(third[1], sums[0, 2][:, HALF:J], 2, one_pick[2][:, HALF:J])
+        for h, queue in enumerate((nc.scalar, nc.sync)):
+            finish(result[3][:, halves[h]], tile3[:, halves[h]], two_picks[3][:, halves[h]], 3, h * HALF, queue)
+        finish(result[2][:, HALF:J], tile2[:, HALF:J], third[1], 2, HALF, nc.scalar)

@@ -74,14 +74,14 @@ def tile_list_max_bias_kernel(tc, xT, wgt, w_words, w_scales, b, offs, out):
 
         def column(i, c, j):
             if c == LATE:
-                c, j = (1, j) if i < 2 else (1 - j // HALF, j % HALF)
-            return i * EARLY + c * J + j
+                return (3 + i) * J + j
+            return i * EARLY + (1 - c if i == 3 else c) * J + j
 
         codes = [keep.tile([P, J], U32, name=f"codes{c}", align_bytes=64) for c in range(PICKS)]
         scales = [keep.tile([P, J], U8, name=f"scales{c}", align_bytes=64) for c in range(PICKS)]
-        one_pick = [late_room[:, HALF:HALF + J] if m == 2 else keep.tile([P, J], F32, name=f"one_pick{m}")[:]
-                    for m in range(N_TILES)]
-        two_picks = [keep.tile([P, J], F32, name=f"two_picks{m}")[:] for m in range(N_TILES)]
+        one_pick = [keep.tile([P, J], F32, name=f"one_pick{m}")[:] for m in range(N_TILES)]
+        two_picks = [products[:, column(0, LATE, 0) - HALF:column(0, LATE, HALF)] if m == 1
+                     else keep.tile([P, J], F32, name=f"two_picks{m}")[:] for m in range(N_TILES)]
         result = [keep.tile([P, J], F32, name=f"result{m}")[:] for m in range(N_TILES)]
         sums = {}
 
@@ -94,9 +94,16 @@ def tile_list_max_bias_kernel(tc, xT, wgt, w_words, w_scales, b, offs, out):
 
         def interleave(c, i0, j0, j1):
             first = column(i0, c, j0)
-            src = products[:, first:first + 2 * EARLY].rearrange("p (i e) -> p e i", i=2)[:, 0:j1 - j0, :]
+            pitch = column(i0 + 1, c, j0) - first
+            src = products[:, first:first + 2 * pitch].rearrange("p (i e) -> p e i", i=2)[:, 0:j1 - j0, :]
             dst = grouped[c].rearrange("p (j i) -> p j i", i=PACK)[:, j0:j1, i0:i0 + 2]
-            nc.scalar.activation(dst, src, ACT.Copy, scale=-1.0 if c == 1 else 1.0)
+            nc.scalar.activation(dst, src, ACT.Copy, scale=-1.0 if c == 0 else 1.0)
+
+        def interleave_late(j0, j1):
+            first = column(0, LATE, 0)
+            src = products[:, first:first + PACK * J].rearrange("p (i q r) -> p q i r", i=PACK, r=4)[:, j0 // 4:j1 // 4]
+            dst = grouped[LATE][:, PACK * j0:PACK * j1].rearrange("p (q r i) -> p q i r", i=PACK, r=4)
+            nc.scalar.copy(dst, src)
 
         def quantize(c, j0, j1):
             nc.vector.quantize_mx(out=codes[c][:, j0:j1].bitcast(FP8X4), scales=scales[c][:, j0:j1],
@@ -112,13 +119,13 @@ def tile_list_max_bias_kernel(tc, xT, wgt, w_words, w_scales, b, offs, out):
             project(sums[c, m], c, m, 0, J)
 
         def move_first(m):
-            nc.scalar.activation(one_pick[m], sums[1, m], ACT.Identity, bias=bias[:, m:m + 1], scale=-1.0)
+            nc.scalar.activation(one_pick[m], sums[0, m], ACT.Identity, bias=bias[:, m:m + 1], scale=-1.0)
 
         def pool(dst, src, m, so_far):
             nc.vector.scalar_tensor_tensor(dst, src, bias[:, m:m + 1], so_far, ALU.add, ALU.max)
 
         def pool_early(m):
-            pool(two_picks[m], sums[0, m], m, one_pick[m])
+            pool(two_picks[m], sums[1, m], m, one_pick[m])
 
         def finish(dst, src, so_far, m, j0, queue):
             pool(dst, src, m, so_far)
@@ -126,66 +133,64 @@ def tile_list_max_bias_kernel(tc, xT, wgt, w_words, w_scales, b, offs, out):
 
         gather(0, 0, 0, EARLY)
         gather(1, 0, 0, EARLY)
-        for c in (1, 0):
+        for c in range(LATE):
             interleave(c, 0, 0, J)
         gather(2, 0, 0, EARLY)
-        for c in (1, 0):
+        for c in range(LATE):
             gather(3, c, 0, J)
             interleave(c, 2, 0, J)
-        for i in range(2):
-            gather(i, LATE, 0, J)
-        interleave(LATE, 0, 0, J)
+        gather(0, LATE, 0, J)
+        quantize(0, 0, J)
+        for m in range(3):
+            project_early(0, m, m)
+        gather(1, LATE, 0, J)
         quantize(1, 0, J)
         for m in range(3):
-            project_early(1, m, m)
+            project_early(1, m, N_TILES + m)
+            move_first(m)
+        lead = psum.tile([P, J], F32, name="bank3")
+        project(lead[:], 1, 3, 0, J, stop=False)
+        project(lead[:], 0, 3, 0, J, start=False)
         for i in (2, 3):
             gather(i, LATE, 0, HALF)
-        move_first(0)
-        interleave(LATE, 2, 0, HALF)
-        quantize(0, 0, J)
-        for m in range(N_TILES - 1):
-            project_early(0, m, N_TILES + m)
-        for i in (2, 3):
-            gather(i, LATE, HALF, J)
-        move_first(1)
-        lead = psum.tile([P, J], F32, name="bank1")
-        project(lead[:], 0, 3, 0, J, stop=False)
-        project(lead[:], 1, 3, 0, J, start=False)
-        interleave(LATE, 2, HALF, J)
-        move_first(2)
+        interleave_late(0, HALF)
+        gather(2, LATE, HALF, J)
+        for j0 in (HALF, HALF + HALF // 2):
+            gather(3, LATE, j0, j0 + HALF // 2)
+            interleave_late(j0, j0 + HALF // 2)
 
+        pool_early(0)
+        project_early(0, 3, N_TILES)
         quantize(LATE, 0, HALF)
         first_halves = psum.tile([P, J], F32, name="bank0")
         for m in range(2):
             project(first_halves[:, m * HALF:(m + 1) * HALF], LATE, m, 0, HALF)
-        tile2 = psum.tile([P, J], F32, name="bank7")
-        pool_early(0)
-        project_early(1, 3, N_TILES)
-        gain = [keep.tile([P, HALF], F32, name="gain")[:], grouped[LATE][:, PACK * HALF:PACK * HALF + J].bitcast(F32)]
+        gain = [late_room[:, J - HALF // 2:J + HALF // 2], grouped[LATE][:, PACK * HALF:PACK * HALF + J].bitcast(F32)]
         halves = [slice(h * HALF, (h + 1) * HALF) for h in range(2)]
         pool_early(1)
         quantize(LATE, HALF, J)
         for h, places in enumerate(halves):
             nc.scalar.activation(gain[h], lead[:, places], ACT.Relu)
-            nc.scalar.activation(one_pick[3][:, places], sums[1, 3][:, places], ACT.Identity, bias=bias[:, 3:4],
+            nc.scalar.activation(one_pick[3][:, places], sums[0, 3][:, places], ACT.Identity, bias=bias[:, 3:4],
                                  scale=-1.0)
             nc.gpsimd.tensor_tensor(two_picks[3][:, places], gain[h], one_pick[3][:, places], ALU.add)
-        second_halves = psum.tile([P, J], F32, name="bank2")
+        second_halves = psum.tile([P, J], F32, name="bank1")
         for m in range(2):
             project(second_halves[:, m * HALF:(m + 1) * HALF], LATE, m, HALF, J)
+        tile2 = psum.tile([P, J], F32, name="bank7")
         project(tile2[:], LATE, 2, 0, J)
-        tile3 = psum.tile([P, J], F32, name="bank4")
+        tile3 = psum.tile([P, J], F32, name="bank2")
         project(tile3[:], LATE, 3, 0, J)
         for m in range(2):
             start = column(2 + m, LATE, HALF)
             finish(products[:, start:start + HALF], first_halves[:, m * HALF:(m + 1) * HALF],
                    two_picks[m][:, 0:HALF], m, 0, nc.sync)
-        third = (two_picks[2][:, 0:HALF], two_picks[0][:, HALF:J])
-        pool(third[0], sums[0, 2][:, 0:HALF], 2, one_pick[2][:, 0:HALF])
+        third = (products[:, column(1, LATE, HALF):column(1, LATE, J)], two_picks[0][:, HALF:J])
+        pool(third[0], sums[1, 2][:, 0:HALF], 2, one_pick[2][:, 0:HALF])
         for m, queue in enumerate((nc.sync, nc.scalar)):
             finish(result[m][:, HALF:J], second_halves[:, halves[m]], two_picks[m][:, HALF:J], m, HALF, queue)
         finish(result[2][:, 0:HALF], tile2[:, 0:HALF], third[0], 2, 0, nc.sync)
-        pool(third[1], sums[0, 2][:, HALF:J], 2, one_pick[2][:, HALF:J])
+        pool(third[1], sums[1, 2][:, HALF:J], 2, one_pick[2][:, HALF:J])
         for h, queue in enumerate((nc.scalar, nc.sync)):
             finish(result[3][:, halves[h]], tile3[:, halves[h]], two_picks[3][:, halves[h]], 3, h * HALF, queue)
         finish(result[2][:, HALF:J], tile2[:, HALF:J], third[1], 2, HALF, nc.scalar)

@@ -21,7 +21,10 @@ PACK = 4
 GROUP = 16
 BLOCK = 32
 N_TILES = N // P
+LAST = N_TILES - 1
+SPLIT = N_TILES - 2
 HALF = J // 2
+QUARTER = J // 4
 LATE = 2
 EARLY = LATE * J
 
@@ -38,7 +41,7 @@ def tile_list_max_bias_kernel(tc, xT, wgt, w_words, w_scales, b, offs, out):
 
         products = keep.tile([P, (PACK + 1) * EARLY], F32, name="products")
         weight_early = keep.tile([P, EARLY], F32, name="weight_early", align_bytes=64)
-        late_room = keep.tile([P, J + HALF], F32, name="late_room")
+        late_room = keep.tile([P, J + QUARTER], F32, name="late_room")
         weight_late = late_room[:, 0:J]
         grouped = [keep.tile([P, PACK * J], BF16, name=f"grouped{c}", align_bytes=64)[:] for c in range(PICKS)]
 
@@ -79,11 +82,20 @@ def tile_list_max_bias_kernel(tc, xT, wgt, w_words, w_scales, b, offs, out):
 
         codes = [keep.tile([P, J], U32, name=f"codes{c}", align_bytes=64) for c in range(PICKS)]
         scales = [keep.tile([P, J], U8, name=f"scales{c}", align_bytes=64) for c in range(PICKS)]
+        halves = [slice(h * HALF, (h + 1) * HALF) for h in range(2)]
         one_pick = [keep.tile([P, J], F32, name=f"one_pick{m}")[:] for m in range(N_TILES)]
-        two_picks = [products[:, column(0, LATE, 0) - HALF:column(0, LATE, HALF)] if m == 1
-                     else keep.tile([P, J], F32, name=f"two_picks{m}")[:] for m in range(N_TILES)]
-        result = [keep.tile([P, J], F32, name=f"result{m}")[:] for m in range(N_TILES)]
-        sums = {}
+        pooled = {
+            0: keep.tile([P, J], F32, name="two_picks0")[:],
+            1: products[:, column(0, LATE, 0) - HALF:column(0, LATE, HALF)],
+            LAST: keep.tile([P, J], F32, name="two_picks3")[:],
+        }
+        two_picks = {m: [whole[:, places] for places in halves] for m, whole in pooled.items()}
+        two_picks[SPLIT] = [products[:, column(1, LATE, HALF):column(1, LATE, J)], two_picks[0][1]]
+        result = {(m, h): products[:, column(2 + m, LATE, HALF):column(2 + m, LATE, J)] if (h == 0 and m < SPLIT)
+                  else keep.tile([P, HALF], F32, name=f"result{m}_{h}")[:]
+                  for m in range(N_TILES) for h in range(2)}
+        early_sums = {}
+        late_sums = {}
 
         def gather(i, c, j0, j1):
             weight = weight_late if c == LATE else weight_early[:, c * J:EARLY]
@@ -92,18 +104,18 @@ def tile_list_max_bias_kernel(tc, xT, wgt, w_words, w_scales, b, offs, out):
                                     plane[i][:].indirect(offsets[:, e0 // GROUP:e1 // GROUP]),
                                     weight[:, j0:j1], ALU.mult)
 
-        def interleave(c, i0, j0, j1):
-            first = column(i0, c, j0)
-            pitch = column(i0 + 1, c, j0) - first
-            src = products[:, first:first + 2 * pitch].rearrange("p (i e) -> p e i", i=2)[:, 0:j1 - j0, :]
-            dst = grouped[c].rearrange("p (j i) -> p j i", i=PACK)[:, j0:j1, i0:i0 + 2]
+        def interleave_pair(c, i0):
+            first = column(i0, c, 0)
+            pitch = column(i0 + 1, c, 0) - first
+            src = products[:, first:first + 2 * pitch].rearrange("p (i e) -> p e i", i=2)[:, 0:J, :]
+            dst = grouped[c].rearrange("p (j i) -> p j i", i=PACK)[:, :, i0:i0 + 2]
             nc.scalar.activation(dst, src, ACT.Copy, scale=-1.0 if c == 0 else 1.0)
 
         def interleave_late(j0, j1):
             first = column(0, LATE, 0)
-            src = products[:, first:first + PACK * J].rearrange("p (i q r) -> p q i r", i=PACK, r=4)[:, j0 // 4:j1 // 4]
+            src = products[:, first:first + PACK * J].rearrange("p (i q r) -> p q i r", i=PACK, r=4)
             dst = grouped[LATE][:, PACK * j0:PACK * j1].rearrange("p (q r i) -> p q i r", i=PACK, r=4)
-            nc.scalar.copy(dst, src)
+            nc.scalar.copy(dst, src[:, j0 // 4:j1 // 4])
 
         def quantize(c, j0, j1):
             nc.vector.quantize_mx(out=codes[c][:, j0:j1].bitcast(FP8X4), scales=scales[c][:, j0:j1],
@@ -114,83 +126,94 @@ def tile_list_max_bias_kernel(tc, xT, wgt, w_words, w_scales, b, offs, out):
                                 lhsT_scale=w_scale[:, P * m:P * (m + 1)], rhs=codes[c][:, j0:j1].bitcast(FP8X4),
                                 rhs_scale=scales[c][:, j0:j1], start=start, stop=stop)
 
-        def project_early(c, m, bank):
-            sums[c, m] = psum.tile([P, J], F32, name=f"bank{bank}")[:]
-            project(sums[c, m], c, m, 0, J)
+        def bank(number):
+            room = psum.tile([P, J], F32, name=f"bank{number}")
+            return room[:]
 
-        def move_first(m):
-            nc.scalar.activation(one_pick[m], sums[0, m], ACT.Identity, bias=bias[:, m:m + 1], scale=-1.0)
+        def project_early(c, m, number):
+            early_sums[c, m] = bank(number)
+            project(early_sums[c, m], c, m, 0, J)
 
-        def pool(dst, src, m, so_far):
-            nc.vector.scalar_tensor_tensor(dst, src, bias[:, m:m + 1], so_far, ALU.add, ALU.max)
+        def project_late_half(h, number):
+            room = bank(number)
+            for m in range(SPLIT):
+                late_sums[m, h] = room[:, halves[m]]
+                project(late_sums[m, h], LATE, m, h * HALF, (h + 1) * HALF)
+
+        def project_late_whole(m, number):
+            room = bank(number)
+            project(room, LATE, m, 0, J)
+            for h in range(2):
+                late_sums[m, h] = room[:, halves[h]]
+
+        def move_first(m, places):
+            nc.scalar.activation(one_pick[m][:, places], early_sums[0, m][:, places], ACT.Identity,
+                                 bias=bias[:, m:m + 1], scale=-1.0)
+
+        def pool(dst, sums, m, so_far):
+            nc.vector.scalar_tensor_tensor(dst, sums, bias[:, m:m + 1], so_far, ALU.add, ALU.max)
 
         def pool_early(m):
-            pool(two_picks[m], sums[1, m], m, one_pick[m])
+            pool(pooled[m], early_sums[1, m], m, one_pick[m])
 
-        def finish(dst, src, so_far, m, j0, queue):
-            pool(dst, src, m, so_far)
-            queue.dma_start(out[P * m:P * (m + 1), j0:j0 + HALF], dst)
+        def pool_split(h):
+            pool(two_picks[SPLIT][h], early_sums[1, SPLIT][:, halves[h]], SPLIT, one_pick[SPLIT][:, halves[h]])
+
+        def finish(m, h, queue):
+            pool(result[m, h], late_sums[m, h], m, two_picks[m][h])
+            queue.dma_start(out[P * m:P * (m + 1), halves[h]], result[m, h])
 
         gather(0, 0, 0, EARLY)
         gather(1, 0, 0, EARLY)
         for c in range(LATE):
-            interleave(c, 0, 0, J)
+            interleave_pair(c, 0)
         gather(2, 0, 0, EARLY)
         for c in range(LATE):
             gather(3, c, 0, J)
-            interleave(c, 2, 0, J)
+            interleave_pair(c, 2)
+
         gather(0, LATE, 0, J)
         quantize(0, 0, J)
-        for m in range(3):
+        for m in range(LAST):
             project_early(0, m, m)
         gather(1, LATE, 0, J)
         quantize(1, 0, J)
-        for m in range(3):
+        for m in range(LAST):
             project_early(1, m, N_TILES + m)
-            move_first(m)
-        lead = psum.tile([P, J], F32, name="bank3")
-        project(lead[:], 1, 3, 0, J, stop=False)
-        project(lead[:], 0, 3, 0, J, start=False)
+            move_first(m, slice(0, J))
+        lead = bank(3)
+        project(lead, 1, LAST, 0, J, stop=False)
+        project(lead, 0, LAST, 0, J, start=False)
+
         for i in (2, 3):
             gather(i, LATE, 0, HALF)
         interleave_late(0, HALF)
         gather(2, LATE, HALF, J)
-        for j0 in (HALF, HALF + HALF // 2):
-            gather(3, LATE, j0, j0 + HALF // 2)
-            interleave_late(j0, j0 + HALF // 2)
+        for j0 in (HALF, HALF + QUARTER):
+            gather(3, LATE, j0, j0 + QUARTER)
+            interleave_late(j0, j0 + QUARTER)
 
         pool_early(0)
-        project_early(0, 3, N_TILES)
+        project_early(0, LAST, N_TILES)
         quantize(LATE, 0, HALF)
-        first_halves = psum.tile([P, J], F32, name="bank0")
-        for m in range(2):
-            project(first_halves[:, m * HALF:(m + 1) * HALF], LATE, m, 0, HALF)
-        gain = [late_room[:, J - HALF // 2:J + HALF // 2], grouped[LATE][:, PACK * HALF:PACK * HALF + J].bitcast(F32)]
-        halves = [slice(h * HALF, (h + 1) * HALF) for h in range(2)]
+        project_late_half(0, 0)
         pool_early(1)
         quantize(LATE, HALF, J)
-        for h, places in enumerate(halves):
-            nc.scalar.activation(gain[h], lead[:, places], ACT.Relu)
-            nc.scalar.activation(one_pick[3][:, places], sums[0, 3][:, places], ACT.Identity, bias=bias[:, 3:4],
-                                 scale=-1.0)
-            nc.gpsimd.tensor_tensor(two_picks[3][:, places], gain[h], one_pick[3][:, places], ALU.add)
-        second_halves = psum.tile([P, J], F32, name="bank1")
-        for m in range(2):
-            project(second_halves[:, m * HALF:(m + 1) * HALF], LATE, m, HALF, J)
-        tile2 = psum.tile([P, J], F32, name="bank7")
-        project(tile2[:], LATE, 2, 0, J)
-        tile3 = psum.tile([P, J], F32, name="bank2")
-        project(tile3[:], LATE, 3, 0, J)
-        for m in range(2):
-            start = column(2 + m, LATE, HALF)
-            finish(products[:, start:start + HALF], first_halves[:, m * HALF:(m + 1) * HALF],
-                   two_picks[m][:, 0:HALF], m, 0, nc.sync)
-        third = (products[:, column(1, LATE, HALF):column(1, LATE, J)], two_picks[0][:, HALF:J])
-        pool(third[0], sums[1, 2][:, 0:HALF], 2, one_pick[2][:, 0:HALF])
-        for m, queue in enumerate((nc.sync, nc.scalar)):
-            finish(result[m][:, HALF:J], second_halves[:, halves[m]], two_picks[m][:, HALF:J], m, HALF, queue)
-        finish(result[2][:, 0:HALF], tile2[:, 0:HALF], third[0], 2, 0, nc.sync)
-        pool(third[1], sums[1, 2][:, HALF:J], 2, one_pick[2][:, HALF:J])
-        for h, queue in enumerate((nc.scalar, nc.sync)):
-            finish(result[3][:, halves[h]], tile3[:, halves[h]], two_picks[3][:, halves[h]], 3, h * HALF, queue)
-        finish(result[2][:, HALF:J], tile2[:, HALF:J], third[1], 2, HALF, nc.scalar)
+
+        gain = [late_room[:, J - QUARTER:J + QUARTER], grouped[LATE][:, PACK * HALF:PACK * HALF + J].bitcast(F32)]
+        for h in range(2):
+            nc.scalar.activation(gain[h], lead[:, halves[h]], ACT.Relu)
+            move_first(LAST, halves[h])
+            nc.gpsimd.tensor_tensor(two_picks[LAST][h], gain[h], one_pick[LAST][:, halves[h]], ALU.add)
+        project_late_half(1, 1)
+        project_late_whole(SPLIT, 7)
+        project_late_whole(LAST, 2)
+
+        for m in range(SPLIT):
+            finish(m, 0, nc.sync)
+        pool_split(0)
+        for m, h in ((0, 1), (1, 1), (SPLIT, 0)):
+            finish(m, h, nc.sync)
+        pool_split(1)
+        for m, h in ((LAST, 0), (LAST, 1), (SPLIT, 1)):
+            finish(m, h, nc.sync)

@@ -52,9 +52,8 @@ def tile_list_max_bias_kernel(tc, xT, wgt, w_words, w_scales, b, offs, out):
 
         x_planes = xT.rearrange("(p i) t -> p i t", i=PACK)
         plane = [keep.tile([P, T], F32, name=f"plane{i}") for i in range(PACK)]
-        nc.sync.dma_start(plane[0][:], x_planes[:, 0, :])
         nc.sync.dma_start(offsets[:], offs)
-        for i in range(1, PACK):
+        for i in range(PACK):
             nc.sync.dma_start(plane[i][:], x_planes[:, i, :])
         nc.sync.dma_start(weight_late, wgt[:, EARLY:PICKS * J])
         w_codes = keep.tile([P, 2 * N], U8, name="w_codes", align_bytes=64)

@@ -133,17 +133,11 @@ def tile_list_max_bias_kernel(tc, xT, wgt, w_words, w_scales, b, offs, out):
             early_sums[c, m] = bank(number)
             project(early_sums[c, m], c, m, 0, J)
 
-        def project_late_half(h, number):
+        def project_late(h, first, number):
             room = bank(number)
-            for m in range(SPLIT):
-                late_sums[m, h] = room[:, halves[m]]
-                project(late_sums[m, h], LATE, m, h * HALF, (h + 1) * HALF)
-
-        def project_late_whole(m, number):
-            room = bank(number)
-            project(room, LATE, m, 0, J)
-            for h in range(2):
-                late_sums[m, h] = room[:, halves[h]]
+            for side in range(2):
+                late_sums[first + side, h] = room[:, halves[side]]
+                project(late_sums[first + side, h], LATE, first + side, h * HALF, (h + 1) * HALF)
 
         def move_first(m, places):
             nc.scalar.activation(one_pick[m][:, places], early_sums[0, m][:, places], ACT.Identity,
@@ -195,7 +189,8 @@ def tile_list_max_bias_kernel(tc, xT, wgt, w_words, w_scales, b, offs, out):
         pool_early(0)
         project_early(0, LAST, N_TILES)
         quantize(LATE, 0, HALF)
-        project_late_half(0, 0)
+        project_late(0, 0, 0)
+        project_late(0, SPLIT, 1)
         pool_early(1)
         quantize(LATE, HALF, J)
 
@@ -204,9 +199,8 @@ def tile_list_max_bias_kernel(tc, xT, wgt, w_words, w_scales, b, offs, out):
             nc.scalar.activation(gain[h], lead[:, halves[h]], ACT.Relu)
             move_first(LAST, halves[h])
             nc.gpsimd.tensor_tensor(two_picks[LAST][h], gain[h], one_pick[LAST][:, halves[h]], ALU.add)
-        project_late_half(1, 1)
-        project_late_whole(SPLIT, 7)
-        project_late_whole(LAST, 2)
+        project_late(1, 0, 2)
+        project_late(1, SPLIT, 7)
 
         for m in range(SPLIT):
             finish(m, 0, nc.sync)

@@ -41,9 +41,9 @@ def tile_list_max_bias_kernel(tc, xT, wgt, w_words, w_scales, b, offs, out):
 
         products = keep.tile([P, (PACK + 1) * EARLY], F32, name="products")
         weight_early = keep.tile([P, EARLY], F32, name="weight_early", align_bytes=64)
-        late_room = keep.tile([P, J + QUARTER], F32, name="late_room")
-        weight_late = late_room[:, 0:J]
-        grouped = [keep.tile([P, PACK * J], BF16, name=f"grouped{c}", align_bytes=64)[:] for c in range(PICKS)]
+        weight_late = keep.tile([P, J], F32, name="weight_late")[:]
+        grouped = [keep.tile([P, PACK * J], BF16, name=f"grouped{c}", align_bytes=64)[:] for c in range(LATE)]
+        late_grouped = {1: keep.tile([P, PACK * HALF], BF16, name="late_grouped1", align_bytes=64)[:]}
 
         dealt = keep.tile([P, LATE * BLOCK], F32, name="dealt", align_bytes=64)
         turned = keep.tile([P, LATE * BLOCK], F32, name="turned", align_bytes=64)
@@ -83,16 +83,21 @@ def tile_list_max_bias_kernel(tc, xT, wgt, w_words, w_scales, b, offs, out):
         scales = [keep.tile([P, J], U8, name=f"scales{c}", align_bytes=64) for c in range(PICKS)]
         halves = [slice(h * HALF, (h + 1) * HALF) for h in range(2)]
         one_pick = [keep.tile([P, J], F32, name=f"one_pick{m}")[:] for m in range(N_TILES)]
-        pooled = {
-            0: keep.tile([P, J], F32, name="two_picks0")[:],
-            1: products[:, column(0, LATE, 0) - HALF:column(0, LATE, HALF)],
-            LAST: keep.tile([P, J], F32, name="two_picks3")[:],
-        }
-        two_picks = {m: [whole[:, places] for places in halves] for m, whole in pooled.items()}
-        two_picks[SPLIT] = [products[:, column(1, LATE, HALF):column(1, LATE, J)], two_picks[0][1]]
-        result = {(m, h): products[:, column(2 + m, LATE, HALF):column(2 + m, LATE, J)] if (h == 0 and m < SPLIT)
+
+        def late_products(i, h):
+            return products[:, column(i, LATE, h * HALF):column(i, LATE, (h + 1) * HALF)]
+
+        def late_input(h):
+            return late_grouped[h][:, 0:J].bitcast(F32)
+
+        two_picks = {(m, 0): late_products(m, 0) for m in range(LAST)}
+        two_picks[0, 1] = late_products(0, 1)
+        two_picks[1, 1] = two_picks[SPLIT, 0]
+        two_picks[SPLIT, 1] = two_picks[0, 1]
+        result = {(m, h): late_products(m, 1) if (h == 0 and m >= SPLIT)
                   else keep.tile([P, HALF], F32, name=f"result{m}_{h}")[:]
                   for m in range(N_TILES) for h in range(2)}
+        gain = [keep.tile([P, HALF], F32, name=f"gain{h}")[:] for h in range(2)]
         early_sums = {}
         late_sums = {}
 
@@ -113,12 +118,13 @@ def tile_list_max_bias_kernel(tc, xT, wgt, w_words, w_scales, b, offs, out):
         def interleave_late(j0, j1):
             first = column(0, LATE, 0)
             src = products[:, first:first + PACK * J].rearrange("p (i q r) -> p q i r", i=PACK, r=4)
-            dst = grouped[LATE][:, PACK * j0:PACK * j1].rearrange("p (q r i) -> p q i r", i=PACK, r=4)
+            h = j0 // HALF
+            dst = late_grouped[h][:, PACK * (j0 - h * HALF):PACK * (j1 - h * HALF)].rearrange("p (q r i) -> p q i r", i=PACK, r=4)
             nc.scalar.copy(dst, src[:, j0 // 4:j1 // 4])
 
         def quantize(c, j0, j1):
             nc.vector.quantize_mx(out=codes[c][:, j0:j1].bitcast(FP8X4), scales=scales[c][:, j0:j1],
-                                  in_=grouped[c][:, PACK * j0:PACK * j1])
+                                  in_=late_grouped[j0 // HALF] if c == LATE else grouped[c])
 
         def project(dst, c, m, j0, j1, start=True, stop=True):
             nc.tensor.matmul_mx(out=dst, lhsT=w_codes[:, 2 * P * m:2 * P * (m + 1)].bitcast(FP4X4),
@@ -146,15 +152,19 @@ def tile_list_max_bias_kernel(tc, xT, wgt, w_words, w_scales, b, offs, out):
         def pool(dst, sums, m, so_far):
             nc.vector.scalar_tensor_tensor(dst, sums, bias[:, m:m + 1], so_far, ALU.add, ALU.max)
 
-        def pool_early(m):
-            pool(pooled[m], early_sums[1, m], m, one_pick[m])
+        def pool_early(m, h):
+            pool(two_picks[m, h], early_sums[1, m][:, halves[h]], m, one_pick[m][:, halves[h]])
 
-        def pool_split(h):
-            pool(two_picks[SPLIT][h], early_sums[1, SPLIT][:, halves[h]], SPLIT, one_pick[SPLIT][:, halves[h]])
+        def pool_off_vector(h):
+            nc.scalar.activation(gain[h], lead[:, halves[h]], ACT.Relu, scale=-1.0)
+            nc.scalar.activation(one_pick[LAST][:, halves[h]], early_sums[1, LAST][:, halves[h]], ACT.Identity,
+                                 bias=bias[:, LAST:LAST + 1])
+            two_picks[LAST, h] = late_input(h)
+            return lambda: nc.gpsimd.tensor_tensor(two_picks[LAST, h], gain[h], one_pick[LAST][:, halves[h]], ALU.add)
 
-        def finish(m, h, queue):
-            pool(result[m, h], late_sums[m, h], m, two_picks[m][h])
-            queue.dma_start(out[P * m:P * (m + 1), halves[h]], result[m, h])
+        def finish(m, h):
+            pool(result[m, h], late_sums[m, h], m, two_picks[m, h])
+            nc.sync.dma_start(out[P * m:P * (m + 1), halves[h]], result[m, h])
 
         gather(0, 0, 0, EARLY)
         gather(1, 0, 0, EARLY)
@@ -169,44 +179,44 @@ def tile_list_max_bias_kernel(tc, xT, wgt, w_words, w_scales, b, offs, out):
         quantize(0, 0, J)
         for m in range(LAST):
             project_early(0, m, m)
-        gather(1, LATE, 0, J)
-        quantize(1, 0, J)
-        for m in range(LAST):
-            project_early(1, m, N_TILES + m)
             move_first(m, slice(0, J))
         lead = bank(3)
-        project(lead, 1, LAST, 0, J, stop=False)
-        project(lead, 0, LAST, 0, J, start=False)
-
+        project(lead, 0, LAST, 0, J, stop=False)
+        gather(1, LATE, 0, J)
         for i in (2, 3):
             gather(i, LATE, 0, HALF)
+        late_grouped[0] = keep.tile([P, PACK * HALF], BF16, name="codes0", align_bytes=64)[:]
         interleave_late(0, HALF)
+        quantize(1, 0, J)
+        project(lead, 1, LAST, 0, J, start=False)
+        project_early(1, LAST, 7)
+        for m in range(LAST):
+            project_early(1, m, N_TILES + m)
+        add_first = pool_off_vector(0)
         gather(2, LATE, HALF, J)
         for j0 in (HALF, HALF + QUARTER):
             gather(3, LATE, j0, j0 + QUARTER)
             interleave_late(j0, j0 + QUARTER)
+        add_second = pool_off_vector(1)
 
-        pool_early(0)
-        project_early(0, LAST, N_TILES)
         quantize(LATE, 0, HALF)
+        add_first()
         project_late(0, 0, 0)
         project_late(0, SPLIT, 1)
-        pool_early(1)
+        for m in range(LAST):
+            pool_early(m, 0)
+        finish(0, 0)
+        finish(1, 0)
         quantize(LATE, HALF, J)
-
-        gain = [late_room[:, J - QUARTER:J + QUARTER], grouped[LATE][:, PACK * HALF:PACK * HALF + J].bitcast(F32)]
-        for h in range(2):
-            nc.scalar.activation(gain[h], lead[:, halves[h]], ACT.Relu)
-            move_first(LAST, halves[h])
-            nc.gpsimd.tensor_tensor(two_picks[LAST][h], gain[h], one_pick[LAST][:, halves[h]], ALU.add)
+        add_second()
         project_late(1, 0, 2)
-        project_late(1, SPLIT, 7)
-
-        for m in range(SPLIT):
-            finish(m, 0, nc.sync)
-        pool_split(0)
-        for m, h in ((0, 1), (1, 1), (SPLIT, 0)):
-            finish(m, h, nc.sync)
-        pool_split(1)
-        for m, h in ((LAST, 0), (LAST, 1), (SPLIT, 1)):
-            finish(m, h, nc.sync)
+        project_late(1, SPLIT, 3)
+        finish(SPLIT, 0)
+        pool_early(0, 1)
+        finish(LAST, 0)
+        pool_early(1, 1)
+        finish(0, 1)
+        finish(LAST, 1)
+        pool_early(SPLIT, 1)
+        finish(1, 1)
+        finish(SPLIT, 1)

@@ -39,7 +39,7 @@ def tile_list_max_bias_kernel(tc, xT, wgt, w_words, w_scales, b, offs, out):
         w_scale = keep.tile([P, N], U8, name="w_scale", align_bytes=64)
         nc.gpsimd.memset(w_scale[:].bitcast(I32), 0)
 
-        products = keep.tile([P, (PACK + 1) * EARLY], F32, name="products")
+        products = keep.tile([P, 2 * EARLY + 9 * HALF + J], F32, name="products")
         weight_early = keep.tile([P, EARLY], F32, name="weight_early", align_bytes=64)
         weight_late = keep.tile([P, J], F32, name="weight_late")[:]
         grouped = [keep.tile([P, PACK * J], BF16, name=f"grouped{c}", align_bytes=64)[:] for c in range(LATE)]
@@ -75,9 +75,16 @@ def tile_list_max_bias_kernel(tc, xT, wgt, w_words, w_scales, b, offs, out):
             nc.vector.transpose(weight_early[:, c * J:(c + 1) * J], spread[c][:])
 
         def column(i, c, j):
+            h, first, second = j // HALF, 2 * EARLY, 2 * EARLY + 5 * HALF
             if c == LATE:
-                return (3 + i) * J + j
-            return i * EARLY + (1 - c if i == 3 else c) * J + j
+                return (first, second)[h] + i * HALF + j % HALF
+            if i < 2:
+                return i * EARLY + c * J + j
+            if c == 1:
+                return second + (i - 2) * J + j
+            if i == 2:
+                return first + QUARTER + j
+            return first + (4 - h) * HALF + j % HALF
 
         codes = [keep.tile([P, J], U32, name=f"codes{c}", align_bytes=64) for c in range(PICKS)]
         scales = [keep.tile([P, J], U8, name=f"scales{c}", align_bytes=64) for c in range(PICKS)]
@@ -85,14 +92,15 @@ def tile_list_max_bias_kernel(tc, xT, wgt, w_words, w_scales, b, offs, out):
         one_pick = [keep.tile([P, J], F32, name=f"one_pick{m}")[:] for m in range(N_TILES)]
 
         def late_products(i, h):
-            return products[:, column(i, LATE, h * HALF):column(i, LATE, (h + 1) * HALF)]
+            return products[:, column(i, LATE, h * HALF):column(i, LATE, h * HALF) + HALF]
 
         def late_input(h):
             return late_grouped[h][:, 0:J].bitcast(F32)
 
-        two_picks = {(m, 0): late_products(m, 0) for m in range(LAST)}
-        two_picks[0, 1] = late_products(0, 1)
-        two_picks[1, 1] = two_picks[SPLIT, 0]
+        two_picks = {(m, 0): late_products(m, 0) for m in range(1, LAST)}
+        two_picks[0, 0] = keep.tile([P, HALF], F32, name="two_picks0")[:]
+        two_picks[0, 1] = late_products(0, 0)
+        two_picks[1, 1] = late_products(0, 1)
         two_picks[SPLIT, 1] = two_picks[0, 1]
         result = {(m, h): late_products(m, 1) if (h == 0 and m >= SPLIT)
                   else keep.tile([P, HALF], F32, name=f"result{m}_{h}")[:]
@@ -108,19 +116,20 @@ def tile_list_max_bias_kernel(tc, xT, wgt, w_words, w_scales, b, offs, out):
                                     plane[i][:].indirect(offsets[:, e0 // GROUP:e1 // GROUP]),
                                     weight[:, j0:j1], ALU.mult)
 
-        def interleave_pair(c, i0):
-            first = column(i0, c, 0)
-            pitch = column(i0 + 1, c, 0) - first
-            src = products[:, first:first + 2 * pitch].rearrange("p (i e) -> p e i", i=2)[:, 0:J, :]
-            dst = grouped[c].rearrange("p (j i) -> p j i", i=PACK)[:, :, i0:i0 + 2]
+        def interleave_pair(c, i0, j0, j1):
+            first = column(i0, c, j0)
+            pitch = column(i0 + 1, c, j0) - first
+            src = products[:, first:first + 2 * pitch].rearrange("p (i e) -> p e i", i=2)[:, 0:j1 - j0, :]
+            dst = grouped[c].rearrange("p (j i) -> p j i", i=PACK)[:, j0:j1, i0:i0 + 2]
             nc.scalar.activation(dst, src, ACT.Copy, scale=-1.0 if c == 0 else 1.0)
 
         def interleave_late(j0, j1):
-            first = column(0, LATE, 0)
-            src = products[:, first:first + PACK * J].rearrange("p (i q r) -> p q i r", i=PACK, r=4)
             h = j0 // HALF
-            dst = late_grouped[h][:, PACK * (j0 - h * HALF):PACK * (j1 - h * HALF)].rearrange("p (q r i) -> p q i r", i=PACK, r=4)
-            nc.scalar.copy(dst, src[:, j0 // 4:j1 // 4])
+            first = column(0, LATE, h * HALF)
+            src = products[:, first:first + PACK * HALF].rearrange("p (i q r) -> p q i r", i=PACK, r=4)
+            dst = late_grouped[h].rearrange("p (q r i) -> p q i r", i=PACK, r=4)
+            places = slice((j0 - h * HALF) // 4, (j1 - h * HALF) // 4)
+            nc.scalar.copy(dst[:, places], src[:, places])
 
         def quantize(c, j0, j1):
             nc.vector.quantize_mx(out=codes[c][:, j0:j1].bitcast(FP8X4), scales=scales[c][:, j0:j1],
@@ -167,23 +176,25 @@ def tile_list_max_bias_kernel(tc, xT, wgt, w_words, w_scales, b, offs, out):
             nc.sync.dma_start(out[P * m:P * (m + 1), halves[h]], result[m, h])
 
         gather(0, 0, 0, EARLY)
-        gather(1, 0, 0, EARLY)
         for c in range(LATE):
-            interleave_pair(c, 0)
-        gather(2, 0, 0, EARLY)
+            gather(1, c, 0, J)
+            interleave_pair(c, 0, 0, J)
         for c in range(LATE):
-            gather(3, c, 0, J)
-            interleave_pair(c, 2)
+            gather(2, c, 0, J)
+        for j0 in (0, HALF):
+            gather(3, 0, j0, j0 + HALF)
+            interleave_pair(0, 2, j0, j0 + HALF)
+        gather(3, 1, 0, J)
+        interleave_pair(1, 2, 0, J)
 
-        gather(0, LATE, 0, J)
+        gather(0, LATE, 0, HALF)
         quantize(0, 0, J)
         for m in range(LAST):
             project_early(0, m, m)
             move_first(m, slice(0, J))
         lead = bank(3)
         project(lead, 0, LAST, 0, J, stop=False)
-        gather(1, LATE, 0, J)
-        for i in (2, 3):
+        for i in (1, 2, 3):
             gather(i, LATE, 0, HALF)
         late_grouped[0] = keep.tile([P, PACK * HALF], BF16, name="codes0", align_bytes=64)[:]
         interleave_late(0, HALF)
@@ -193,18 +204,21 @@ def tile_list_max_bias_kernel(tc, xT, wgt, w_words, w_scales, b, offs, out):
         for m in range(LAST):
             project_early(1, m, N_TILES + m)
         add_first = pool_off_vector(0)
-        gather(2, LATE, HALF, J)
+        for i in (0, 1, 2):
+            gather(i, LATE, HALF, J)
         for j0 in (HALF, HALF + QUARTER):
             gather(3, LATE, j0, j0 + QUARTER)
             interleave_late(j0, j0 + QUARTER)
         add_second = pool_off_vector(1)
 
+        pool_early(0, 0)
         quantize(LATE, 0, HALF)
         add_first()
         project_late(0, 0, 0)
         project_late(0, SPLIT, 1)
-        for m in range(LAST):
-            pool_early(m, 0)
+        pool_early(1, 0)
+        pool_early(SPLIT, 0)
+        pool_early(0, 1)
         finish(0, 0)
         finish(1, 0)
         quantize(LATE, HALF, J)
@@ -212,9 +226,8 @@ def tile_list_max_bias_kernel(tc, xT, wgt, w_words, w_scales, b, offs, out):
         project_late(1, 0, 2)
         project_late(1, SPLIT, 3)
         finish(SPLIT, 0)
-        pool_early(0, 1)
-        finish(LAST, 0)
         pool_early(1, 1)
+        finish(LAST, 0)
         finish(0, 1)
         finish(LAST, 1)
         pool_early(SPLIT, 1)

@@ -27,6 +27,7 @@ HALF = J // 2
 QUARTER = J // 4
 LATE = 2
 EARLY = LATE * J
+LATE_PITCH = J + QUARTER
 
 
 def tile_list_max_bias_kernel(tc, xT, wgt, w_words, w_scales, b, offs, out):
@@ -39,9 +40,8 @@ def tile_list_max_bias_kernel(tc, xT, wgt, w_words, w_scales, b, offs, out):
         w_scale = keep.tile([P, N], U8, name="w_scale", align_bytes=64)
         nc.gpsimd.memset(w_scale[:].bitcast(I32), 0)
 
-        products = keep.tile([P, 2 * EARLY + 9 * HALF + J], F32, name="products")
-        weight_early = keep.tile([P, EARLY], F32, name="weight_early", align_bytes=64)
-        weight_late = keep.tile([P, J], F32, name="weight_late")[:]
+        products = keep.tile([P, 10 * LATE_PITCH], F32, name="products")
+        weight = keep.tile([P, PICKS * J], F32, name="weight", align_bytes=64)
         grouped = [keep.tile([P, PACK * J], BF16, name=f"grouped{c}", align_bytes=64)[:] for c in range(LATE)]
         late_grouped = {1: keep.tile([P, PACK * HALF], BF16, name="late_grouped1", align_bytes=64)[:]}
 
@@ -55,7 +55,7 @@ def tile_list_max_bias_kernel(tc, xT, wgt, w_words, w_scales, b, offs, out):
         nc.sync.dma_start(offsets[:], offs)
         for i in range(PACK):
             nc.sync.dma_start(plane[i][:], x_planes[:, i, :])
-        nc.sync.dma_start(weight_late, wgt[:, EARLY:PICKS * J])
+        nc.sync.dma_start(weight[:, EARLY:PICKS * J], wgt[:, EARLY:PICKS * J])
         w_codes = keep.tile([P, 2 * N], U8, name="w_codes", align_bytes=64)
         nc.sync.dma_start(w_codes[:].bitcast(I32), w_words[0].bitcast(I32))
         for quadrant in range(4):
@@ -72,19 +72,14 @@ def tile_list_max_bias_kernel(tc, xT, wgt, w_words, w_scales, b, offs, out):
             src = turned[:].rearrange("p (u h r) -> p r u h", u=LATE, h=2)[:, c * runs:(c + 1) * runs]
             copy(spread[c][:].rearrange("p (r u h s) -> p r u h s", u=LATE, h=2, s=GROUP),
                  src.unsqueeze(4).to_broadcast([P, runs, LATE, 2, GROUP]))
-            nc.vector.transpose(weight_early[:, c * J:(c + 1) * J], spread[c][:])
+            nc.vector.transpose(weight[:, c * J:(c + 1) * J], spread[c][:])
 
         def column(i, c, j):
-            h, first, second = j // HALF, 2 * EARLY, 2 * EARLY + 5 * HALF
             if c == LATE:
-                return (first, second)[h] + i * HALF + j % HALF
-            if i < 2:
-                return i * EARLY + c * J + j
-            if c == 1:
-                return second + (i - 2) * J + j
-            if i == 2:
-                return first + QUARTER + j
-            return first + (4 - h) * HALF + j % HALF
+                return 2 * EARLY + HALF + (i - 1) * LATE_PITCH + j
+            if i == 3:
+                return (4 * EARLY, 3 * EARLY)[c] + j
+            return i * EARLY + c * J + j
 
         codes = [keep.tile([P, J], U32, name=f"codes{c}", align_bytes=64) for c in range(PICKS)]
         scales = [keep.tile([P, J], U8, name=f"scales{c}", align_bytes=64) for c in range(PICKS)]
@@ -95,13 +90,13 @@ def tile_list_max_bias_kernel(tc, xT, wgt, w_words, w_scales, b, offs, out):
             return products[:, column(i, LATE, h * HALF):column(i, LATE, h * HALF) + HALF]
 
         def late_input(h):
-            return late_grouped[h][:, 0:J].bitcast(F32)
+            return late_grouped[1][:, h * J:(h + 1) * J].bitcast(F32)
 
         two_picks = {(m, 0): late_products(m, 0) for m in range(1, LAST)}
         two_picks[0, 0] = keep.tile([P, HALF], F32, name="two_picks0")[:]
         two_picks[0, 1] = late_products(0, 0)
         two_picks[1, 1] = late_products(0, 1)
-        two_picks[SPLIT, 1] = two_picks[0, 1]
+        two_picks[SPLIT, 1] = late_products(1, 1)
         result = {(m, h): late_products(m, 1) if (h == 0 and m >= SPLIT)
                   else keep.tile([P, HALF], F32, name=f"result{m}_{h}")[:]
                   for m in range(N_TILES) for h in range(2)}
@@ -110,11 +105,10 @@ def tile_list_max_bias_kernel(tc, xT, wgt, w_words, w_scales, b, offs, out):
         late_sums = {}
 
         def gather(i, c, j0, j1):
-            weight = weight_late if c == LATE else weight_early[:, c * J:EARLY]
             e0, e1 = c * J + j0, c * J + j1
             nc.vector.tensor_tensor(products[:, column(i, c, j0):column(i, c, j0) + j1 - j0],
                                     plane[i][:].indirect(offsets[:, e0 // GROUP:e1 // GROUP]),
-                                    weight[:, j0:j1], ALU.mult)
+                                    weight[:, e0:e1], ALU.mult)
 
         def interleave_pair(c, i0, j0, j1):
             first = column(i0, c, j0)
@@ -126,7 +120,8 @@ def tile_list_max_bias_kernel(tc, xT, wgt, w_words, w_scales, b, offs, out):
         def interleave_late(j0, j1):
             h = j0 // HALF
             first = column(0, LATE, h * HALF)
-            src = products[:, first:first + PACK * HALF].rearrange("p (i q r) -> p q i r", i=PACK, r=4)
+            pitch = column(1, LATE, h * HALF) - first
+            src = products[:, first:first + PACK * pitch].rearrange("p (i q r) -> p q i r", i=PACK, r=4)
             dst = late_grouped[h].rearrange("p (q r i) -> p q i r", i=PACK, r=4)
             places = slice((j0 - h * HALF) // 4, (j1 - h * HALF) // 4)
             nc.scalar.copy(dst[:, places], src[:, places])
@@ -176,44 +171,39 @@ def tile_list_max_bias_kernel(tc, xT, wgt, w_words, w_scales, b, offs, out):
             nc.sync.dma_start(out[P * m:P * (m + 1), halves[h]], result[m, h])
 
         gather(0, 0, 0, EARLY)
+        gather(1, 0, 0, EARLY)
         for c in range(LATE):
-            gather(1, c, 0, J)
             interleave_pair(c, 0, 0, J)
-        for c in range(LATE):
-            gather(2, c, 0, J)
-        for j0 in (0, HALF):
-            gather(3, 0, j0, j0 + HALF)
-            interleave_pair(0, 2, j0, j0 + HALF)
-        gather(3, 1, 0, J)
+        gather(2, 0, 0, EARLY)
+        gather(3, 0, 0, J)
+        interleave_pair(0, 2, 0, J)
+        gather(3, 1, 0, EARLY)
         interleave_pair(1, 2, 0, J)
 
-        gather(0, LATE, 0, HALF)
         quantize(0, 0, J)
         for m in range(LAST):
             project_early(0, m, m)
             move_first(m, slice(0, J))
         lead = bank(3)
         project(lead, 0, LAST, 0, J, stop=False)
-        for i in (1, 2, 3):
+        gather(0, LATE, 0, J)
+        for i in (1, 2):
             gather(i, LATE, 0, HALF)
         late_grouped[0] = keep.tile([P, PACK * HALF], BF16, name="codes0", align_bytes=64)[:]
         interleave_late(0, HALF)
         quantize(1, 0, J)
-        project(lead, 1, LAST, 0, J, start=False)
-        project_early(1, LAST, 7)
         for m in range(LAST):
             project_early(1, m, N_TILES + m)
-        add_first = pool_off_vector(0)
-        for i in (0, 1, 2):
+        project(lead, 1, LAST, 0, J, start=False)
+        project_early(1, LAST, 7)
+        for i in (1, 2):
             gather(i, LATE, HALF, J)
-        for j0 in (HALF, HALF + QUARTER):
-            gather(3, LATE, j0, j0 + QUARTER)
-            interleave_late(j0, j0 + QUARTER)
+        interleave_late(HALF, J)
+        add_first = pool_off_vector(0)
         add_second = pool_off_vector(1)
 
         pool_early(0, 0)
         quantize(LATE, 0, HALF)
-        add_first()
         project_late(0, 0, 0)
         project_late(0, SPLIT, 1)
         pool_early(1, 0)
@@ -222,14 +212,15 @@ def tile_list_max_bias_kernel(tc, xT, wgt, w_words, w_scales, b, offs, out):
         finish(0, 0)
         finish(1, 0)
         quantize(LATE, HALF, J)
+        add_first()
         add_second()
         project_late(1, 0, 2)
         project_late(1, SPLIT, 3)
         finish(SPLIT, 0)
         pool_early(1, 1)
-        finish(LAST, 0)
-        finish(0, 1)
-        finish(LAST, 1)
         pool_early(SPLIT, 1)
+        finish(0, 1)
+        finish(LAST, 0)
         finish(1, 1)
         finish(SPLIT, 1)
+        finish(LAST, 1)

@@ -183,6 +183,7 @@ def tile_list_max_bias_kernel(tc, xT, wgt, w_words, w_scales, b, offs, out):
         quantize(0, 0, J)
         for m in range(LAST):
             project_early(0, m, m)
+        for m in range(SPLIT):
             move_first(m, slice(0, J))
         lead = bank(3)
         project(lead, 0, LAST, 0, J, stop=False)
@@ -191,6 +192,7 @@ def tile_list_max_bias_kernel(tc, xT, wgt, w_words, w_scales, b, offs, out):
             gather(i, LATE, 0, HALF)
         late_grouped[0] = keep.tile([P, PACK * HALF], BF16, name="codes0", align_bytes=64)[:]
         interleave_late(0, HALF)
+        move_first(SPLIT, slice(0, J))
         quantize(1, 0, J)
         for m in range(LAST):
             project_early(1, m, N_TILES + m)

@@ -43,7 +43,9 @@ def tile_list_max_bias_kernel(tc, xT, wgt, w_words, w_scales, b, offs, out):
         products = keep.tile([P, 10 * LATE_PITCH], F32, name="products")
         weight = keep.tile([P, PICKS * J], F32, name="weight", align_bytes=64)
         grouped = [keep.tile([P, PACK * J], BF16, name=f"grouped{c}", align_bytes=64)[:] for c in range(LATE)]
-        late_grouped = {1: keep.tile([P, PACK * HALF], BF16, name="late_grouped1", align_bytes=64)[:]}
+        late_grouped = [keep.tile([P, PACK * HALF], BF16, name=f"late_grouped{h}", align_bytes=64)[:] for h in range(2)]
+        minus_one = late_grouped[0][:, 0:2].bitcast(F32)
+        nc.gpsimd.memset(minus_one, -1.0)
 
         dealt = keep.tile([P, LATE * BLOCK], F32, name="dealt", align_bytes=64)
         turned = keep.tile([P, LATE * BLOCK], F32, name="turned", align_bytes=64)
@@ -151,7 +153,7 @@ def tile_list_max_bias_kernel(tc, xT, wgt, w_words, w_scales, b, offs, out):
 
         def move_first(m, places):
             nc.scalar.activation(one_pick[m][:, places], early_sums[0, m][:, places], ACT.Identity,
-                                 bias=bias[:, m:m + 1], scale=-1.0)
+                                 bias=bias[:, m:m + 1], scale=minus_one if m == 0 else -1.0)
 
         def pool(dst, sums, m, so_far):
             nc.vector.scalar_tensor_tensor(dst, sums, bias[:, m:m + 1], so_far, ALU.add, ALU.max)
@@ -190,7 +192,6 @@ def tile_list_max_bias_kernel(tc, xT, wgt, w_words, w_scales, b, offs, out):
         gather(0, LATE, 0, J)
         for i in (1, 2):
             gather(i, LATE, 0, HALF)
-        late_grouped[0] = keep.tile([P, PACK * HALF], BF16, name="codes0", align_bytes=64)[:]
         interleave_late(0, HALF)
         move_first(SPLIT, slice(0, J))
         quantize(1, 0, J)

@@ -92,15 +92,16 @@ def tile_list_max_bias_kernel(tc, xT, wgt, w_words, w_scales, b, offs, out):
             return products[:, column(i, LATE, h * HALF):column(i, LATE, h * HALF) + HALF]
 
         def late_input(h):
-            return late_grouped[1][:, h * J:(h + 1) * J].bitcast(F32)
+            return late_grouped[h][:, J:2 * J].bitcast(F32)
 
-        two_picks = {(m, 0): late_products(m, 0) for m in range(1, LAST)}
+        second_tile = products[:, column(0, LATE, 0) - HALF:column(0, LATE, HALF)]
+        two_picks = {(1, h): second_tile[:, halves[h]] for h in range(2)}
         two_picks[0, 0] = keep.tile([P, HALF], F32, name="two_picks0")[:]
-        two_picks[0, 1] = late_products(0, 0)
-        two_picks[1, 1] = late_products(0, 1)
-        two_picks[SPLIT, 1] = late_products(1, 1)
-        result = {(m, h): late_products(m, 1) if (h == 0 and m >= SPLIT)
-                  else keep.tile([P, HALF], F32, name=f"result{m}_{h}")[:]
+        two_picks[0, 1] = late_products(1, 0)
+        two_picks[SPLIT, 0] = late_products(1, 1)
+        two_picks[SPLIT, 1] = two_picks[0, 1]
+        held = {(1, 0): late_products(2, 1), (LAST, 0): late_products(3, 1)}
+        result = {(m, h): held[m, h] if (m, h) in held else keep.tile([P, HALF], F32, name=f"result{m}_{h}")[:]
                   for m in range(N_TILES) for h in range(2)}
         gain = [keep.tile([P, HALF], F32, name=f"gain{h}")[:] for h in range(2)]
         early_sums = {}
@@ -162,9 +163,8 @@ def tile_list_max_bias_kernel(tc, xT, wgt, w_words, w_scales, b, offs, out):
             pool(two_picks[m, h], early_sums[1, m][:, halves[h]], m, one_pick[m][:, halves[h]])
 
         def pool_off_vector(h):
-            nc.scalar.activation(gain[h], lead[:, halves[h]], ACT.Relu, scale=-1.0)
-            nc.scalar.activation(one_pick[LAST][:, halves[h]], early_sums[1, LAST][:, halves[h]], ACT.Identity,
-                                 bias=bias[:, LAST:LAST + 1])
+            move_first(LAST, halves[h])
+            nc.scalar.activation(gain[h], lead[:, halves[h]], ACT.Relu)
             two_picks[LAST, h] = late_input(h)
             return lambda: nc.gpsimd.tensor_tensor(two_picks[LAST, h], gain[h], one_pick[LAST][:, halves[h]], ALU.add)
 
@@ -189,41 +189,41 @@ def tile_list_max_bias_kernel(tc, xT, wgt, w_words, w_scales, b, offs, out):
             move_first(m, slice(0, J))
         lead = bank(3)
         project(lead, 0, LAST, 0, J, stop=False)
+        project_early(0, LAST, 7)
         gather(0, LATE, 0, J)
         for i in (1, 2):
             gather(i, LATE, 0, HALF)
         interleave_late(0, HALF)
-        move_first(SPLIT, slice(0, J))
         quantize(1, 0, J)
-        for m in range(LAST):
-            project_early(1, m, N_TILES + m)
+        project_early(1, 0, N_TILES)
         project(lead, 1, LAST, 0, J, start=False)
-        project_early(1, LAST, 7)
+        for m in (1, SPLIT):
+            project_early(1, m, N_TILES + m)
+        add_first = pool_off_vector(0)
         for i in (1, 2):
             gather(i, LATE, HALF, J)
         interleave_late(HALF, J)
-        add_first = pool_off_vector(0)
+        move_first(SPLIT, slice(0, J))
         add_second = pool_off_vector(1)
 
         pool_early(0, 0)
         quantize(LATE, 0, HALF)
+        add_first()
         project_late(0, 0, 0)
         project_late(0, SPLIT, 1)
-        pool_early(1, 0)
-        pool_early(SPLIT, 0)
+        pool(second_tile, early_sums[1, 1], 1, one_pick[1])
         pool_early(0, 1)
         finish(0, 0)
-        finish(1, 0)
         quantize(LATE, HALF, J)
-        add_first()
         add_second()
-        project_late(1, 0, 2)
-        project_late(1, SPLIT, 3)
-        finish(SPLIT, 0)
-        pool_early(1, 1)
-        pool_early(SPLIT, 1)
-        finish(0, 1)
+        project_late(1, 0, 4)
+        project_late(1, SPLIT, 5)
+        finish(1, 0)
         finish(LAST, 0)
+        pool_early(SPLIT, 0)
+        finish(0, 1)
+        finish(SPLIT, 0)
         finish(1, 1)
-        finish(SPLIT, 1)
+        pool_early(SPLIT, 1)
         finish(LAST, 1)
+        finish(SPLIT, 1)

@@ -41,7 +41,8 @@ def tile_list_max_bias_kernel(tc, xT, wgt, w_words, w_scales, b, offs, out):
         nc.gpsimd.memset(w_scale[:].bitcast(I32), 0)
 
         products = keep.tile([P, 10 * LATE_PITCH], F32, name="products")
-        weight = keep.tile([P, PICKS * J], F32, name="weight", align_bytes=64)
+        weight_room = keep.tile([P, PICKS * J + 2 * BLOCK], F32, name="weight", align_bytes=64)
+        weight = weight_room[:, BLOCK:BLOCK + PICKS * J]
         grouped = [keep.tile([P, PACK * J], BF16, name=f"grouped{c}", align_bytes=64)[:] for c in range(LATE)]
         late_grouped = [keep.tile([P, PACK * HALF], BF16, name=f"late_grouped{h}", align_bytes=64)[:] for h in range(2)]
         minus_one = late_grouped[0][:, 0:2].bitcast(F32)

from contextlib import ExitStack

import concourse.mybir as mybir

K, N, T, J, PICKS = 512, 512, 2048, 512, 3
FLOPS = 2 * K * N * J * PICKS

F32 = mybir.dt.float32
BF16 = mybir.dt.bfloat16
I32 = mybir.dt.int32
U32 = mybir.dt.uint32
U16 = mybir.dt.uint16
U8 = mybir.dt.uint8
FP8X4 = mybir.dt.float8_e4m3fn_x4
FP4X4 = mybir.dt.float4_e2m1fn_x4
ALU = mybir.AluOpType
ACT = mybir.ActivationFunctionType

P = 128
PACK = 4
GROUP = 16
BLOCK = 32
N_TILES = N // P
LAST = N_TILES - 1
SPLIT = N_TILES - 2
HALF = J // 2
QUARTER = J // 4
LATE = 2
EARLY = LATE * J
LATE_PITCH = J + QUARTER


def tile_list_max_bias_kernel(tc, xT, wgt, w_words, w_scales, b, offs, out):
    nc = tc.nc
    with ExitStack() as ctx:
        keep = ctx.enter_context(tc.tile_pool(name="keep", bufs=1))
        psum = ctx.enter_context(tc.psum_pool(name="psum", bufs=1))

        offsets = keep.tile([P, PICKS * J // GROUP], U16, name="offsets")
        w_scale = keep.tile([P, N], U8, name="w_scale", align_bytes=64)
        nc.gpsimd.memset(w_scale[:].bitcast(I32), 0)

        products = keep.tile([P, 10 * LATE_PITCH], F32, name="products")
        weight_room = keep.tile([P, PICKS * J + 2 * BLOCK], F32, name="weight", align_bytes=64)
        weight = weight_room[:, BLOCK:BLOCK + PICKS * J]
        grouped = [keep.tile([P, PACK * J], BF16, name=f"grouped{c}", align_bytes=64)[:] for c in range(LATE)]
        late_grouped = [keep.tile([P, PACK * HALF], BF16, name=f"late_grouped{h}", align_bytes=64)[:] for h in range(2)]
        minus_one = late_grouped[0][:, 0:2].bitcast(F32)
        nc.gpsimd.memset(minus_one, -1.0)

        dealt = keep.tile([P, LATE * BLOCK], F32, name="dealt", align_bytes=64)
        turned = keep.tile([P, LATE * BLOCK], F32, name="turned", align_bytes=64)
        spread = [keep.tile([P, J], F32, name=f"spread{c}", align_bytes=64) for c in range(LATE)]
        nc.sync.dma_start(dealt[:], wgt[0:P:GROUP, 0:EARLY].rearrange("g (r e) -> g r e", r=GROUP))

        x_planes = xT.rearrange("(p i) t -> p i t", i=PACK)
        plane = [keep.tile([P, T], F32, name=f"plane{i}") for i in range(PACK)]
        nc.sync.dma_start(offsets[:], offs)
        for i in range(PACK):
            nc.sync.dma_start(plane[i][:], x_planes[:, i, :])
        nc.sync.dma_start(weight[:, EARLY:PICKS * J], wgt[:, EARLY:PICKS * J])
        w_codes = keep.tile([P, 2 * N], U8, name="w_codes", align_bytes=64)
        nc.sync.dma_start(w_codes[:].bitcast(I32), w_words[0].bitcast(I32))
        for quadrant in range(4):
            nc.sync.dma_start(w_scale[32 * quadrant:32 * quadrant + 4, :].bitcast(I32),
                              w_scales[0, 4 * quadrant:4 * quadrant + 4, :].bitcast(I32))
        bias = keep.tile([P, N_TILES], F32, name="bias")
        with nc.allow_non_contiguous_dma(reason="one bias value a partition"):
            nc.sync.dma_start(bias[:], b.rearrange("(m p) -> p m", p=P))

        for u in range(LATE):
            nc.vector.transpose(turned[:, u * BLOCK:(u + 1) * BLOCK], dealt[:, u * BLOCK:(u + 1) * BLOCK])
        runs = GROUP // LATE
        for c, copy in enumerate((nc.vector.tensor_copy, nc.scalar.copy)):
            src = turned[:].rearrange("p (u h r) -> p r u h", u=LATE, h=2)[:, c * runs:(c + 1) * runs]
            copy(spread[c][:].rearrange("p (r u h s) -> p r u h s", u=LATE, h=2, s=GROUP),
                 src.unsqueeze(4).to_broadcast([P, runs, LATE, 2, GROUP]))
            nc.vector.transpose(weight[:, c * J:(c + 1) * J], spread[c][:])

        def column(i, c, j):
            if c == LATE:
                return 2 * EARLY + HALF + (i - 1) * LATE_PITCH + j
            if i == 3:
                return (4 * EARLY, 3 * EARLY)[c] + j
            return i * EARLY + c * J + j

        codes = [keep.tile([P, J], U32, name=f"codes{c}", align_bytes=64) for c in range(PICKS)]
        scales = [keep.tile([P, J], U8, name=f"scales{c}", align_bytes=64) for c in range(PICKS)]
        halves = [slice(h * HALF, (h + 1) * HALF) for h in range(2)]
        one_pick = [keep.tile([P, J], F32, name=f"one_pick{m}")[:] for m in range(N_TILES)]

        def late_products(i, h):
            return products[:, column(i, LATE, h * HALF):column(i, LATE, h * HALF) + HALF]

        def late_input(h):
            return late_grouped[h][:, J:2 * J].bitcast(F32)

        second_tile = products[:, column(0, LATE, 0) - HALF:column(0, LATE, HALF)]
        two_picks = {(1, h): second_tile[:, halves[h]] for h in range(2)}
        two_picks[0, 0] = keep.tile([P, HALF], F32, name="two_picks0")[:]
        two_picks[0, 1] = late_products(1, 0)
        two_picks[SPLIT, 0] = late_products(1, 1)
        two_picks[SPLIT, 1] = two_picks[0, 1]
        held = {(1, 0): late_products(2, 1), (LAST, 0): late_products(3, 1)}
        result = {(m, h): held[m, h] if (m, h) in held else keep.tile([P, HALF], F32, name=f"result{m}_{h}")[:]
                  for m in range(N_TILES) for h in range(2)}
        gain = [keep.tile([P, HALF], F32, name=f"gain{h}")[:] for h in range(2)]
        early_sums = {}
        late_sums = {}

        def gather(i, c, j0, j1):
            e0, e1 = c * J + j0, c * J + j1
            nc.vector.tensor_tensor(products[:, column(i, c, j0):column(i, c, j0) + j1 - j0],
                                    plane[i][:].indirect(offsets[:, e0 // GROUP:e1 // GROUP]),
                                    weight[:, e0:e1], ALU.mult)

        def interleave_pair(c, i0, j0, j1):
            first = column(i0, c, j0)
            pitch = column(i0 + 1, c, j0) - first
            src = products[:, first:first + 2 * pitch].rearrange("p (i e) -> p e i", i=2)[:, 0:j1 - j0, :]
            dst = grouped[c].rearrange("p (j i) -> p j i", i=PACK)[:, j0:j1, i0:i0 + 2]
            nc.scalar.activation(dst, src, ACT.Copy, scale=-1.0 if c == 0 else 1.0)

        def interleave_late(j0, j1):
            h = j0 // HALF
            first = column(0, LATE, h * HALF)
            pitch = column(1, LATE, h * HALF) - first
            src = products[:, first:first + PACK * pitch].rearrange("p (i q r) -> p q i r", i=PACK, r=4)
            dst = late_grouped[h].rearrange("p (q r i) -> p q i r", i=PACK, r=4)
            places = slice((j0 - h * HALF) // 4, (j1 - h * HALF) // 4)
            nc.scalar.copy(dst[:, places], src[:, places])

        def quantize(c, j0, j1):
            nc.vector.quantize_mx(out=codes[c][:, j0:j1].bitcast(FP8X4), scales=scales[c][:, j0:j1],
                                  in_=late_grouped[j0 // HALF] if c == LATE else grouped[c])

        def project(dst, c, m, j0, j1, start=True, stop=True):
            nc.tensor.matmul_mx(out=dst, lhsT=w_codes[:, 2 * P * m:2 * P * (m + 1)].bitcast(FP4X4),
                                lhsT_scale=w_scale[:, P * m:P * (m + 1)], rhs=codes[c][:, j0:j1].bitcast(FP8X4),
                                rhs_scale=scales[c][:, j0:j1], start=start, stop=stop)

        def bank(number):
            room = psum.tile([P, J], F32, name=f"bank{number}")
            return room[:]

        def project_early(c, m, number):
            early_sums[c, m] = bank(number)
            project(early_sums[c, m], c, m, 0, J)

        def project_late(h, first, number):
            room = bank(number)
            for side in range(2):
                late_sums[first + side, h] = room[:, halves[side]]
                project(late_sums[first + side, h], LATE, first + side, h * HALF, (h + 1) * HALF)

        def move_first(m, places):
            nc.scalar.activation(one_pick[m][:, places], early_sums[0, m][:, places], ACT.Identity,
                                 bias=bias[:, m:m + 1], scale=minus_one if m == 0 else -1.0)

        def pool(dst, sums, m, so_far):
            nc.vector.scalar_tensor_tensor(dst, sums, bias[:, m:m + 1], so_far, ALU.add, ALU.max)

        def pool_early(m, h):
            pool(two_picks[m, h], early_sums[1, m][:, halves[h]], m, one_pick[m][:, halves[h]])

        def pool_off_vector(h):
            move_first(LAST, halves[h])
            nc.scalar.activation(gain[h], lead[:, halves[h]], ACT.Relu)
            two_picks[LAST, h] = late_input(h)
            return lambda: nc.gpsimd.tensor_tensor(two_picks[LAST, h], gain[h], one_pick[LAST][:, halves[h]], ALU.add)

        def finish(m, h):
            pool(result[m, h], late_sums[m, h], m, two_picks[m, h])
            nc.sync.dma_start(out[P * m:P * (m + 1), halves[h]], result[m, h])

        gather(0, 0, 0, EARLY)
        gather(1, 0, 0, EARLY)
        for c in range(LATE):
            interleave_pair(c, 0, 0, J)
        gather(2, 0, 0, EARLY)
        gather(3, 0, 0, J)
        interleave_pair(0, 2, 0, J)
        gather(3, 1, 0, EARLY)
        interleave_pair(1, 2, 0, J)

        quantize(0, 0, J)
        for m in range(LAST):
            project_early(0, m, m)
        for m in range(SPLIT):
            move_first(m, slice(0, J))
        lead = bank(3)
        project(lead, 0, LAST, 0, J, stop=False)
        project_early(0, LAST, 7)
        gather(0, LATE, 0, J)
        for i in (1, 2):
            gather(i, LATE, 0, HALF)
        interleave_late(0, HALF)
        quantize(1, 0, J)
        project_early(1, 0, N_TILES)
        project(lead, 1, LAST, 0, J, start=False)
        for m in (1, SPLIT):
            project_early(1, m, N_TILES + m)
        add_first = pool_off_vector(0)
        for i in (1, 2):
            gather(i, LATE, HALF, J)
        interleave_late(HALF, J)
        move_first(SPLIT, slice(0, J))
        add_second = pool_off_vector(1)

        pool_early(0, 0)
        quantize(LATE, 0, HALF)
        add_first()
        project_late(0, 0, 0)
        project_late(0, SPLIT, 1)
        pool(second_tile, early_sums[1, 1], 1, one_pick[1])
        pool_early(0, 1)
        finish(0, 0)
        quantize(LATE, HALF, J)
        add_second()
        project_late(1, 0, 4)
        project_late(1, SPLIT, 5)
        finish(1, 0)
        finish(LAST, 0)
        pool_early(SPLIT, 0)
        finish(0, 1)
        finish(SPLIT, 0)
        finish(1, 1)
        pool_early(SPLIT, 1)
        finish(LAST, 1)
        finish(SPLIT, 1)
